import numpy as np, ml_dtypes
CORES = [3,11,19,27,35,43,51,59]
N = 8
BF = ml_dtypes.bfloat16
def gentries(a):
    return np.ascontiguousarray(a.reshape(8, 16, -1).transpose(0, 2, 1)).reshape(8, -1)
def gtable(e):
    e = np.asarray(e); return np.ascontiguousarray(e.reshape(8, -1, 16).transpose(0, 2, 1)).reshape(128, -1).astype(np.int32)
XI, M, E, L, S, RO, D = 4096, 2048, 2048, 2048, 256, 2, 4
LB = 11
def forest(rng):
    o = np.argsort(rng.random((N, 8, M)), axis=-1); k = np.arange(M)
    inner = (2 * k + 2 < M) & (rng.random((N, 8, M)) >= 0.12); sw = rng.integers(0, 2, (N, 8, M))
    k0 = np.zeros_like(o); k1 = np.zeros_like(o)
    np.put_along_axis(k0, o, np.take_along_axis(o, np.where(inner, 2 * k + 1 + sw, k), 2), 2)
    np.put_along_axis(k1, o, np.take_along_axis(o, np.where(inner, 2 * k + 2 - sw, k), 2), 2)
    return o, k0, k1
def begin(rng, o, lo, hi):
    lv = rng.integers(lo, hi, (N, 8, L))
    return np.take_along_axis(o, 2 ** lv - 1 + (rng.random((N, 8, L)) * 2 ** lv).astype(np.int64), 2)
def vals(rng, n):
    return rng.integers(0, 256, (N, 8, 16, n))
def parts(rng):
    o, k0, k1 = forest(rng)
    return dict(o=o, x=vals(rng, XI), prev=rng.integers(0, XI, (N, 8, XI)), z=vals(rng, M), rs=vals(rng, M), kid0=k0, kid1=k1, env=vals(rng, E),
                start=begin(rng, o, LB - 3 - D, LB - 1), cur=rng.integers(0, XI, (N, 8, L)), w=rng.integers(1, 128, (N, 8, 16)), th=rng.integers(1000, 1500, (N, 8, 1)))
def pack(d):
    r = {}
    for k in ("x", "prev", "z", "rs", "kid0", "kid1", "env", "start", "cur", "w", "th"):
        if k in ("x", "z", "rs", "env"): r[k] = np.ascontiguousarray(d[k].reshape(N, 128, -1)).astype(np.float32).astype(BF)
        elif k in ("start", "cur"): r[k] = np.stack([gtable(a) for a in d[k]])
        elif k == "w": r[k] = d[k].reshape(N, 128, 1).astype(np.int32)
        else: r[k] = np.ascontiguousarray(d[k]).astype(np.int32)
    return r
def setup_inputs(rng):
    return pack(parts(rng))
def setup_inputs_full(rng):
    d = parts(rng)
    d["start"][:, ::2, :S] = d["o"][:, ::2, M // 2:M // 2 + S]; d["th"][:, ::2] = 0
    d["start"][::2, :, :S] = d["o"][::2, :, M // 2:M // 2 + S]; d["th"][::2] = 0
    return pack(d)
def setup_inputs_ties(rng):
    d = parts(rng)
    for k in ("x", "z", "rs", "env"): d[k] = d[k] // 64 * 64
    d["th"] = 64 * rng.integers(18, 22, (N, 8, 1))
    return pack(d)
def setup_inputs_alike(rng):
    d = parts(rng); m = np.arange(M)
    d["start"][:, 0] = d["o"][:, 0, M - 1:M]; d["th"][:, 0] = 0
    d["start"][:, 1] = rng.choice(np.array([0, M - 1]), (N, L)); d["cur"][:, 1] = rng.choice(np.array([0, XI - 1]), (N, L))
    d["prev"][:, 1] = np.where(rng.random((N, XI)) < 0.5, np.arange(XI), rng.choice(np.array([0, XI - 1]), (N, XI)))
    d["kid0"][:, 2] = (m + 1) & (M - 1); d["kid1"][:, 2] = (m + 1 + rng.integers(0, M - 1, (N, M))) & (M - 1)
    d["kid0"][:, 3] = m; d["kid1"][:, 3] = m
    d["start"][:, 3] = np.take_along_axis(rng.integers(0, M, (N, 40)), rng.integers(0, 40, (N, L)), 1)
    d["w"][:, 4] = 0; d["th"][:, 4] = 4096
    d["z"][:, 5] = 0; d["rs"][:, 5] = rng.choice(np.array([0, 255]), (N, 16, M))
    d["kid1"][:, 6] = d["kid0"][:, 6]; d["prev"][:, 6] = np.arange(XI)
    d["x"][:, 7] = 255; d["env"][:, 7] = 255; d["w"][:, 7] = 127; d["th"][:, 7] = 0
    return pack(d)
def setup_inputs_edges(rng):
    d = parts(rng); r = np.arange(N)[:, None]
    d["start"][:, :2, :S] = d["o"][:, :2, M // 2:M // 2 + S]; d["env"][:, :2] = 0
    c = rng.integers(0, 256, (16, 1)); d["x"][:, 0] = c
    d["rs"][:, 0] = np.where(rng.random((N, 1, M)) < 0.5, c, d["rs"][:, 0]); d["th"][:, 0] = r & 1
    c = 255 * rng.integers(0, 2, (16, 1)); d["x"][:, 1] = c
    d["rs"][:, 1] = 255 - c; d["rs"][:, 1, 0] = np.abs(255 - c[0] - rng.integers(0, 3, (N, M)))
    d["th"][:, 1] = np.array([4080, 4081, 4096, 4079])[r & 3]
    d["x"][:, 2:4] = rng.integers(250, 256, (N, 2, 16, XI)); d["w"][:, 2:4] = 127; d["env"][:, 3] = 0
    d["th"][:, 3] = rng.integers(2040, 2060, (N, 1))
    d["kid1"][:, 4] = np.where(rng.random((N, M)) < 0.5, d["kid0"][:, 4], d["kid1"][:, 4])
    return pack(d)
def setup_inputs_spread(rng):
    d = parts(rng); m = np.arange(M); lf = rng.random((N, 4, M)) < 0.5
    for k in ("kid0", "kid1"): d[k][:, 1::2] = np.where(lf, m, (m + rng.integers(1, M, (N, 4, M))) & (M - 1))
    for k, n in (("x", XI), ("z", M), ("rs", M), ("env", E)):
        d[k] = np.minimum((np.exp2(8 * rng.random((N, 8, 1, n))) * rng.random((N, 8, 16, n))).astype(np.int64), 255)
    d["w"] = np.minimum(np.exp2(7 * rng.random((N, 8, 16))).astype(np.int64), 127)
    d["th"] = np.minimum(np.exp2(12 * rng.random((N, 8, 1))).astype(np.int64), 4096); d["th"][:, 0] = 1; d["th"][:, 1] = 0
    d["start"] = begin(rng, d["o"], 0, LB)
    d["cur"] = np.minimum((XI * rng.random((N, 8, L)) ** 3).astype(np.int64), XI - 1)
    d["prev"] = np.where(rng.random((N, 8, XI)) < 0.5, np.maximum(np.arange(XI) - rng.integers(0, 40, (N, 8, XI)), 0), d["prev"])
    return pack(d)
def check_inputs(d):
    bad = []
    for k, lo, hi in (("x", 0, 255), ("prev", 0, XI - 1), ("z", 0, 255), ("rs", 0, 255), ("kid0", 0, M - 1), ("kid1", 0, M - 1), ("env", 0, 255), ("start", 0, M - 1), ("cur", 0, XI - 1), ("w", 0, 127), ("th", 0, 4096)):
        a = np.asarray(d[k]).astype(np.float32)
        if not np.all((a >= lo) & (a <= hi) & (a == np.floor(a))): bad.append("range of " + k)
    m = np.arange(M)
    if np.any((np.asarray(d["kid0"]) == m) != (np.asarray(d["kid1"]) == m)): bad.append("one kid of a node is the node itself, the other isn't")
    return bad
def pick(a, ix):
    return np.take_along_axis(a, ix[:, :, None, :], 3)
def reference(x, prev, z, rs, kid0, kid1, env, start, cur, w, th):
    def cols(a, more):
        b = a.astype(np.float32).astype(np.int32).reshape(N, 8, 16, -1)
        return np.concatenate([b, np.zeros((N, 8, 16, more), np.int32)], axis=3)
    X = cols(x, RO * L); Z = cols(z, 2 * S * RO); R = cols(rs, 2 * S * RO); EN = cols(env, 0)
    P = np.concatenate([prev.astype(np.int64), np.zeros((N, 8, RO * L), np.int64)], axis=2)
    own = np.zeros((N, 8, 1), np.int64) + np.arange(M, M + 2 * S * RO)
    K0 = np.concatenate([kid0.astype(np.int64), own], axis=2); K1 = np.concatenate([kid1.astype(np.int64), own], axis=2)
    F0 = np.stack([gentries(a) for a in start]).astype(np.int64); C = np.stack([gentries(a) for a in cur]).astype(np.int64)
    W = w.reshape(N, 8, 16, 1).astype(np.int32); TH = th.reshape(N, 8, 1).astype(np.int64)
    lower = np.arange(S)[None, :] < np.arange(S)[:, None]
    for t in range(RO):
        f = F0; s = C
        for step in range(D):
            k0 = np.take_along_axis(K0, f, 2); k1 = np.take_along_axis(K1, f, 2); go = k0 != f
            b = np.sum(pick(X, s) >= pick(Z, f), axis=2) >= 9
            f = np.where(go, np.where(b, k1, k0), f); s = np.where(go, np.take_along_axis(P, s, 2), s)
        xc = pick(X, C); rf = pick(R, f); a = np.sum(rf > xc, axis=2)
        y = pick(EN, (np.sum(W * xc, axis=2) + 97 * a) & (E - 1)); v = (xc + y) & 255
        fs = f[:, :, :S]; leaf = np.take_along_axis(K0, fs, 2) == fs
        first = ~np.any((fs[:, :, :, None] == fs[:, :, None, :]) & lower, axis=3)
        far = np.sum(np.abs(rf[..., :S] - v[..., :S]), axis=2) >= TH
        q, g, i = np.nonzero(leaf & first & far); at = fs[q, g, i]; n0 = M + 2 * S * t + 2 * i; xs = pick(X, s[:, :, :S])
        Z[q, g, :, at] = xs[q, g, :, i]; K0[q, g, at] = n0; K1[q, g, at] = n0 + 1
        R[q, g, :, n0] = rf[q, g, :, i]; R[q, g, :, n0 + 1] = (rf[q, g, :, i] + v[q, g, :, i]) >> 1
        came = np.roll(v, 1, axis=0)
        h = np.sum(W * came, axis=2) & (L - 1); lo = XI + L * t
        X[..., lo:lo + L] = came; P[..., lo:lo + L] = np.take_along_axis(C, h, 2)
        C = np.zeros((N, 8, 1), np.int64) + np.arange(lo, lo + L)
    return {"yk0": K0.astype(np.float32), "yk1": K1.astype(np.float32), "yr": np.ascontiguousarray(R[..., M:].reshape(N, 128, 2 * S * RO)).astype(np.float32).astype(BF), "yp": np.ascontiguousarray(P[..., XI:]).astype(np.float32)}

@@ -1,0 +1,587 @@
+from concourse.bass import DstId, RemoteDMATransfer
+from concourse.mybir import AluOpType as A, ActivationFunctionType as F, AxisListType
+
+S, HL = 256, 1024
+MW = 2560
+DUMP, WW = 3072, 3328
+BIG = 8192.0
+BFB, FP, I4, U2 = "bfloat16", "float32", "int32", "uint16"
+SCRATCH = {}
+
+
+def _decl(where, dtype, text):
+    for w in text.split():
+        nm, c = w.split(":")
+        p = 128
+        if "x" in c:
+            p, c = c.split("x")
+        SCRATCH[nm] = (where, [int(p), int(c)], dtype)
+
+
+_decl("sbuf", BFB, "XW:4096 PW:4096 ZW:3328 KW:3328 RW:2560 EW:2048 OW:2560 HIW:2560 VL:2048 KDl:256 KDh:256 PDl:256 PDh:256 ONB:128 ZB:256 "
+      "IDB:128 IDN:128 I8K:128 BC8:8 SEL:128 BLK:128 MASK:128 EH:16x256 RHS:32 RT:32 OB:128 OBN:128 WQ1:2048 WQP:2048 WQW:2048 WQN:2048 LOI:256 "
+      "HII:256 NK:256 NKb:256 YR1:512 XF:256 PT2:256 RF:256 KQ:256 OQ:256 FBI:256 FE:256 FO:256 LF:256 DUP:16 DUT:16x128 JK:1024 AD:256 SP:256 "
+      "XS0:2048 XS1:2048 XS2:2048 XS3:2048 YS1:2048 YS2:2048 YS3:2048 CK0:2048 CK1:2048 CR0:1024 CR1:1024 PT0:1024 PT1:1024 SS0:1024 SS1:1024 MM0:1024 MM1:1024")
+_decl("sbuf", FP, "KF:3328 CF:2048 HG:2048 thF:8x1 THC:1 KDf:256 cuF:128 cuT:128 ONF:128 IDF:128 E8:8x128 COL:64 DW:16 NV0:256 NV1:256 FW:80 SW:80 "
+      "SFa:64 SFb:64 HR:128 HS:128 DM:16 TG:80 A97:128 MA0:64x128 MA1:64x128 MB0:64x128 MB1:64x128 FT0:64x128 FT1:64x128")
+_decl("sbuf", I4, "stI:128 cuI:128 KD:256 PD:256 wI:1 wN:1 thI:8x1 KDt:256 KDu:256 PDt:256 PDu:256 KI:1 CI:16 FI:256 FB:256 RS1:256 RS2:256 IT:512")
+_decl("sbuf", U2, "LL:1536")
+_decl("psum", FP, "bMI:512 bSP:512 bTP0:512 bTP1:512 bLP0:512 bLP1:512 bOP0:512 bOP1:512")
+SEMAPHORES = ["cv", "cs", "ct", "cg"] + ["d%d" % _k for _k in range(48)] + ["aw", "lw", "aA0", "aA1", "lA0", "lA1", "aH", "lH"]
+
+CYC, GAT = 0.83e-3, 1.56
+WAKE, SELF, DBW, DLAT = 0.12, 0.08, 250.0, 2.0
+MS = ((1, 0), (0, 0))
+ONLY = {"ki": "s", "xs": "s", "pv": "v", "ys": "b", "cu": "s"}
+BETA, TRIES = 0.03, 400
+MODELS = ((1.2, 1.0, 0.12, 1.0, 1.0), (1.2, 0.72, 0.25, 1.5, 1.3), (1.3, 1.25, 0.1, 0.8, 1.0))
+PLANS = {}
+
+
+def make_plan(ops):
+    n = len(ops)
+    succ = [[] for _ in range(n)]
+    for i, o in enumerate(ops):
+        for d in o["deps"]:
+            succ[d].append(i)
+    rq = [[a[0][0] if a[0] in ("yd", "sd", "gr") else a[0] for a in o["alts"]] for o in ops]
+    dma = [o["alts"][0][0] in ("yd", "sd") for o in ops]
+    pri = [0.0] * n
+    for i in range(n - 1, -1, -1):
+        o = ops[i]
+        pri[i] = min(a[1] for a in o["alts"]) + o["lat"] + (DLAT if dma[i] else 0.0) + max([pri[j] + WAKE for j in succ[i]] or [0.0])
+
+    def schedule(boost, pick, beta):
+        left, ready = [len(o["deps"]) for o in ops], [0.0] * n
+        open_ = [i for i in range(n) if not left[i]]
+        free, order, bw = {}, [], 0.0
+        while open_:
+            best = None
+            for i in open_:
+                p = pri[i] + boost[i]
+                for j in range(len(rq[i])):
+                    if pick[i] >= 0 and pick[i] != j:
+                        continue
+                    st = ready[i] if rq[i][j] == "arr" else max(ready[i], free.get(rq[i][j], 0.0))
+                    key = (st - beta * p, -p, i, j)
+                    if best is None or key < best[0]:
+                        best = (key, i, j, st)
+            _, i, j, st = best
+            open_.remove(i)
+            q, d = rq[i][j], ops[i]["alts"][j][1]
+            if q != "arr":
+                free[q] = st + d
+            fin = st + d + ops[i]["lat"]
+            if dma[i]:
+                bw = max(bw, st + d) + ops[i]["lat"]
+                fin = bw + DLAT
+            order.append((i, j))
+            for s_ in succ[i]:
+                ready[s_] = max(ready[s_], fin + (SELF if rq[s_] == [q] else WAKE))
+                left[s_] -= 1
+                if not left[s_]:
+                    open_.append(s_)
+        return order
+
+    def score(order):
+        tot = 0.0
+        for cf, gf, wk, bf, lf in MODELS:
+            fin, free, bw, mx = [0.0] * n, {}, 0.0, 0.0
+            for i, j in order:
+                o, q = ops[i], rq[i][j]
+                d = o["alts"][j][1]
+                if q in "vstg" and not dma[i]:
+                    d *= cf * (gf if o["gat"] else 1.0)
+                t = 0.0 if q == "arr" else free.get(q, 0.0)
+                for x in o["deps"]:
+                    if fin[x] + wk > t:
+                        t = fin[x] + wk
+                e = t + d
+                if q != "arr":
+                    free[q] = e
+                if dma[i]:
+                    bw = max(bw, e) + o["lat"] / bf
+                    e = bw + DLAT * lf
+                else:
+                    e += o["lat"] * lf
+                fin[i] = e
+                mx = max(mx, e)
+            tot += mx / (cf * (1 + gf))
+        return tot
+    boost, pick = [o["boost"] for o in ops], [-1] * n
+    two = [i for i in range(n) if len(rq[i]) == 2]
+    order = schedule(boost, pick, BETA)
+    best, seed = score(order), [7]
+
+    def rnd():
+        seed[0] = (seed[0] * 1103515245 + 12345) % 2147483648
+        return seed[0] / 2147483648.0
+    for it in range(TRIES):
+        b2, p2 = list(boost), list(pick)
+        share, amp = 0.02 + 0.3 * rnd() ** 2, 2.0 + 12.0 * rnd()
+        for i in range(n):
+            if rnd() < share:
+                b2[i] += amp * (2 * rnd() - 1)
+        for i in two:
+            if rnd() < share:
+                p2[i] = int(3 * rnd()) - 1
+        o2 = schedule(b2, p2, BETA)
+        s2 = score(o2)
+        if s2 <= best:
+            best, order, boost, pick = s2, o2, b2, p2
+    return order, best
+
+
+def rank_program(g, core, T, topo):
+    rank = T.rank_of(core)
+    if rank is None:
+        return
+    n_ranks = len(T.cores)
+    nxt, prv = T.cores[(rank + 1) % n_ranks], T.cores[(rank - 1) % n_ranks]
+    ops, last, readers = [], {}, {}
+
+    def LI(k, a, b):
+        return T.LL[:, 128 * k + a:128 * k + b]
+
+    def op(alts, R, W, nm="", lat=0.0, tok=None, boost=0.0, gat=False):
+        i, deps = len(ops), set()
+        for k in list(R) + list(W):
+            if k in last:
+                deps.add(last[k])
+        for k in W:
+            deps.update(readers.get(k, ()))
+        for k in R:
+            readers.setdefault(k, []).append(i)
+        for k in W:
+            last[k] = i
+            readers[k] = []
+        deps.discard(i)
+        ops.append(dict(alts=alts, deps=deps, nm=nm, lat=lat, tok=tok, boost=boost, gat=gat))
+
+    def vc(n, half=False):
+        return 0.05 + max(64, n * (0.5 if half else 1)) * CYC
+
+    def PE(fn, cyc, R, W, nm=""):
+        op([("t", 0.05 + cyc * CYC, fn)], R, W, nm)
+    nd = [0]
+
+    def DMA(out, in_, R, W, nm="", q="y", kb=64, boost=0.0):
+        s = "d%d" % nd[0]
+        nd[0] += 1
+        op([(q + "d", 0.07, lambda e: e.dma_start(out, in_).then_inc(T.sem[s], 16))], R, W, nm, lat=kb / DBW, tok=(s, 16), boost=boost)
+
+    def vcopy(out, in_, R, W, nm=""):
+        op([("v", vc(out.shape[1]), lambda e: e.tensor_copy(out, in_))], R, W, nm)
+
+    def vts(out, in0, s1, s2, o0, o1, R, W, nm="", half=False):
+        if o1 is None:
+            op([("v", vc(out.shape[1], half), lambda e: e.tensor_scalar(out, in0, s1, None, o0))], R, W, nm)
+        else:
+            op([("v", vc(out.shape[1], half), lambda e: e.tensor_scalar(out, in0, s1, s2, o0, o1))], R, W, nm)
+
+    def vtt(out, i0, i1, o, R, W, nm="", two=True):
+        op([("v", vc(out.shape[1] * (2 if two else 1)), lambda e: e.tensor_tensor(out, i0, i1, o))], R, W, nm)
+
+    def act(out, in_, func, R, W, nm="", **k):
+        op([("s", 0.065 + max(64, in_.shape[1]) * CYC, lambda e: e.activation(out, in_, func, **k))], R, W, nm)
+
+    def gather(out, win, off, n, R, W, nm):
+        d = n * GAT * CYC
+        a = [("s", 0.07 + d, lambda e: e.activation(out, win.indirect(off), F.Copy)),
+             ("v", 0.06 + d, lambda e: e.tensor_copy(out, win.indirect(off)))]
+        o_ = ONLY.get(nm[:2], "b")
+        op(a[:1] if o_ == "s" else a[1:] if o_ == "v" else a, R, W, nm, gat=True)
+
+    def gatherop(out, win, off, in1, o, R, W, nm):
+        op([("v", 0.06 + HL * GAT * CYC, lambda e: e.tensor_tensor(out, win.indirect(off), in1, o))], R, W, nm, gat=True)
+
+    def ms(ap, c, W, half=True):
+        op([("v", vc(ap.shape[1], half), lambda e: e.memset(ap, c))], [], W, "ms")
+
+    def cnt_(pat):
+        n = 1
+        for a_, b_ in pat:
+            n *= b_
+        return 0.15 + 2 * n * CYC
+
+    def aff(out, in_, pat, cmpo, fill, base, cm, R, W):
+        op([("g", cnt_(pat), lambda e: e.affine_select(out, in_, pat, cmpo, fill, base, cm))], R, W)
+
+    def iota(out, pat, base, cm, W):
+        op([("g", cnt_(pat), lambda e: e.iota(out, pat, base, cm, allow_small_or_imprecise_dtypes=True))], [], W)
+
+    B = 90.0
+    DMA(T.KD[:, 0:128], T.kid0[:], [], ["KD0"], "kid0", "y", boost=B)
+    DMA(T.PD[:], T.prev[:], [], ["PD"], "prev", "s", 128, boost=B)
+    DMA(T.KD[:, 128:256], T.kid1[:], [], ["KD1"], "kid1", "y", boost=B - 1)
+    DMA(T.cuI[:], T.cur[:], [], ["cuI"], "cur", "s", boost=B - 1)
+    DMA(T.stI[:], T.start[:], [], ["stI"], "start", "y", boost=B - 2)
+    DMA(T.XW[:], T.x[:], [], ["XW"], "x", "s", 1024, boost=B - 2)
+    DMA(T.wI[:], T.w[:], [], ["wI"], "w", "y", 1, boost=B - 3)
+    DMA(T.thI[:], T.th[:], [], ["thI"], "th", "y", 1, boost=B - 7)
+
+    ms(T.ONB[:], 1.0, ["ONB"])
+    ms(T.PW[:], 0.0, ["PW0", "PW1"])
+    ms(T.ONF[:], 1.0, ["ONF"], half=False)
+    ms(T.ZB[:], 0.0, ["ZB"])
+    ms(T.ZW[:, 2048:MW], 0.0, ["ZT"])
+    aff(T.SEL[:], T.ONB[:], [[-1, 16], [-16, 8]], A.is_equal, 0.0, 0, 1, ["ONB"], ["SEL"])
+    aff(T.BC8[:], T.ONB[:, 0:8], [[-16, 8]], A.is_ge, 0.0, 0, 1, ["ONB"], ["BC8"])
+    aff(T.BC8[:], T.BC8[:], [[16, 8]], A.is_ge, 0.0, 15, -1, ["BC8"], ["BC8"])
+    aff(T.IDF[:], T.ONF[:], [[-1, 128]], A.is_equal, 0.0, 0, 1, ["ONF"], ["IDF"])
+    op([("g", 0.2, lambda e: e.iota(T.KI[:], [[0, 1]], 0, 1))], [], ["KI"])
+    aff(T.BLK[:], T.ONB[:], [[-16, 8], [0, 16]], A.is_ge, 0.0, 0, 1, ["ONB"], ["BLK"])
+    aff(T.BLK[:], T.BLK[:], [[16, 8], [0, 16]], A.is_ge, 0.0, 15, -1, ["BLK"], ["BLK"])
+    iota(T.WQP[:], [[0, 2048]], 0, 0, ["WQP"])
+    iota(T.WQ1[:], [[0, 2048]], 0, 0, ["WQ1"])
+    iota(T.OW[:], [[0, 10], [1, 256]], 0, 0, ["OW0", "OW1"])
+    iota(T.HIW[:], [[1, 10], [0, 256]], 0, 0, ["HIW"])
+    aff(T.MASK[:], T.ZB[:, 0:128], [[-1, 128]], A.is_gt, -8.0, 0, 1, ["ZB"], ["MASK"])
+    aff(T.EH[:], T.ZB[0:16, :], [[-8, 2], [-1, 8], [0, 16]], A.not_equal, -BIG, 0, 1, ["ZB"], ["EH"])
+    aff(T.E8[:], T.ONF[0:8, :], [[-1, 8], [0, 16]], A.is_equal, 0.0, 0, 1, ["ONF"], ["E8"])
+    iota(T.DW[:], [[16, 16]], DUMP, 0, ["DW"])
+    iota(T.NV0[:], [[2, 256]], 2048, 0, ["NV0"])
+    iota(T.LOI[:], [[0, 2], [2, 128]], 0, 0, ["LOI"])
+    iota(T.HII[:], [[1, 2], [0, 128]], 8, 0, ["HII"])
+    iota(T.KF[:, 2048:3072], [[1, 1024]], 2048, 0, ["KFt"])
+    iota(T.CF[:], [[0, 2048]], 0, 0, ["CF"])
+    act(T.KW[:, 0:MW], T.PW[:, 0:MW], F.Copy, ["PW0", "PW1"], ["KW0", "KW1", "KW2", "KW3", "KT0", "KT1", "KT2", "KT3"], "kwz")
+
+    C = {}
+
+    def col(nm):
+        C.setdefault(nm, len(C))
+        return T.COL[:, C[nm]:C[nm] + 1]
+
+    def ci(j):
+        return T.CI[:, j:j + 1]
+    vts(ci(8), T.KI[:], 15, None, A.bitwise_and, None, ["KI"], ["KIt"])
+    vcopy(col("k"), ci(8), ["KIt"], ["k"])
+    for c in range(4):
+        vts(col("e%d" % c), col("k"), float(c), None, A.is_equal, None, ["k"], ["e%d" % c])
+    vtt(col("e02"), col("e0"), col("e2"), A.add, ["e0", "e2"], ["e02"])
+    vtt(col("e13"), col("e1"), col("e3"), A.add, ["e1", "e3"], ["e13"])
+    vts(col("p1"), col("e1"), 256.0, None, A.mult, None, ["e1"], ["p1"])
+    vtt(col("pc"), col("e0"), col("p1"), A.add, ["e0", "p1"], ["pc"])
+    vts(col("pn"), col("pc"), -1.0, None, A.mult, None, ["pc"], ["pn"])
+    for j, fac in enumerate((0.5, 0.25, 0.0625, 0.00390625)):
+        b = 1 << j
+        vts(ci(j), ci(8), b, None, A.bitwise_and, None, ["KIt"], ["ci%d" % j])
+        vts(col("s%d" % j), ci(j), (fac - 1.0) / b, 1.0, A.mult, A.add, ["ci%d" % j], ["s%d" % j])
+    vtt(col("s01"), col("s0"), col("s1"), A.mult, ["s0", "s1"], ["s01"])
+    vtt(col("s23"), col("s2"), col("s3"), A.mult, ["s2", "s3"], ["s23"])
+    vtt(col("sp"), col("s01"), col("s23"), A.mult, ["s01", "s23"], ["sp"])
+    vts(col("sc"), col("sp"), 2048.0, None, A.mult, None, ["sp"], ["sc"])
+    vts(ci(4), T.KI[:], 16, None, A.bitwise_and, None, ["KI"], ["ci4"])
+    vts(col("m0"), ci(4), 0.0625, None, A.mult, None, ["ci4"], ["m0"])
+    vts(col("m1"), col("k"), 12.0, -3.75, A.is_ge, A.mult, ["k"], ["m1"])
+    vts(col("m2"), col("m1"), 1.0, None, A.add, None, ["m1"], ["m2"])
+    vtt(col("mo"), col("m0"), col("m2"), A.mult, ["m0", "m2"], ["mo"])
+    vtt(col("me"), col("m2"), col("mo"), A.subtract, ["m2", "mo"], ["me"])
+    ms(col("c85"), -8.5, ["c85"], half=False)
+    vts(T.RT[:, 0:8], T.SEL[:, 8:16], 256.0, None, A.mult, None, ["SEL"], ["t0"])
+    vtt(T.RT[:, 0:8], T.RT[:, 0:8], T.SEL[:, 0:8], A.add, ["t0", "SEL"], ["P01"])
+    vts(T.RT[:, 8:16], T.SEL[:, 24:32], 256.0, None, A.mult, None, ["SEL"], ["t1"])
+    vtt(T.RT[:, 16:24], T.RT[:, 8:16], T.SEL[:, 16:24], A.add, ["t1", "SEL"], ["P23"])
+    vcopy(T.RHS[:, 0:8], T.BC8[:], ["BC8"], ["RHSa"])
+    vtt(T.RHS[:, 8:16], T.RT[:, 16:24], T.RT[:, 0:8], A.add, ["P23", "P01"], ["RHSb"])
+    vtt(T.RHS[:, 16:24], T.RT[:, 16:24], T.RT[:, 0:8], A.subtract, ["P23", "P01"], ["RHSb"])
+    vtt(T.RHS[:, 24:32], T.RT[:, 16:24], T.RT[:, 0:8], A.subtract, ["P23", "P01"], ["RHSd"])
+    vts(T.RHS[:, 8:24], T.RHS[:, 8:24], 0.5, None, A.mult, None, ["RHSb"], ["RHSb"])
+    RH = ["RHSa", "RHSb", "RHSd"]
+
+    def fillq(dst, src, R, W):
+        op([("s", 16 * (0.065 + 64 * CYC), lambda e: [e.activation(dst[:, 129 * q:128 * q + 128:16], src, F.Copy) for q in range(16)])], R + W, W, "fill")
+    fillq(T.WQP, T.RT[:, 0:8], ["P01"], ["WQP"])
+    fillq(T.WQ1, T.BC8[:], ["BC8"], ["WQ1"])
+    vcopy(col("w"), T.wI[:], ["wI"], ["w"])
+    act(T.WQW[:], T.WQ1[:], F.Copy, ["WQ1", "w"], ["WQW"], "WQW", scale=col("w"))
+    vcopy(T.IDB[:], T.IDF[:], ["IDF"], ["IDB"])
+    vts(T.IDN[:], T.IDF[:], -1.0, None, A.mult, None, ["IDF"], ["IDN"])
+    vts(T.I8K[:], T.IDF[:], BIG, None, A.mult, None, ["IDF"], ["I8K"])
+    vts(T.OB[:], T.BLK[:], col("pc"), None, A.mult, None, ["BLK", "pc"], ["OB"], half=True)
+    vts(T.OBN[:], T.BLK[:], col("pn"), None, A.mult, None, ["BLK", "pn"], ["OBN"], half=True)
+    vts(T.DW[:], T.DW[:], col("k"), None, A.add, None, ["DW", "k"], ["DW"])
+    vts(T.NV0[:], T.NV0[:], col("e1"), None, A.add, None, ["NV0", "e1"], ["NV0"])
+    vts(T.NV1[:], T.NV0[:], 512.0, None, A.add, None, ["NV0"], ["NV1"])
+    vts(T.NK[:], T.LOI[:], col("e02"), col("e2"), A.mult, A.add, ["LOI", "e02", "e2"], ["NK"], half=True)
+    vts(T.NKb[:], T.HII[:], col("e13"), None, A.mult, None, ["HII", "e13"], ["NKb"], half=True)
+    vtt(T.NK[:], T.NK[:], T.NKb[:], A.add, ["NK", "NKb"], ["NK"])
+
+    vcopy(LI(0, 0, 128), T.stI[:], ["stI"], ["L0_0", "L0_1"])
+    vcopy(LI(5, 0, 128), T.cuI[:], ["cuI"], ["SL0_0", "SL0_1"])
+    vts(T.PDt[:], T.PD[:], 255, None, A.bitwise_and, None, ["PD"], ["PDt"])
+    vts(T.PDu[:], T.PD[:], 8, None, A.arith_shift_right, None, ["PD"], ["PDu"])
+    vcopy(T.PDl[:], T.PDt[:], ["PDt"], ["PDl"])
+    vcopy(T.PDh[:], T.PDu[:], ["PDu"], ["PDh"])
+    DMA(T.PW[0:128:16, :], T.PDl[:], ["PDl"], ["PW0"], "pw0")
+    DMA(T.PW[1:128:16, :], T.PDh[:], ["PDh"], ["PW1"], "pw1", "s")
+    vts(T.KDt[:], T.KD[:], 255, None, A.bitwise_and, None, ["KD0", "KD1"], ["KDt"])
+    vts(T.KDu[:], T.KD[:], 8, None, A.arith_shift_right, None, ["KD0", "KD1"], ["KDu"])
+    vcopy(T.KDl[:], T.KDt[:], ["KDt"], ["KDl"])
+    vcopy(T.KDh[:], T.KDu[:], ["KDu"], ["KDh"])
+    DMA(T.KW[0:128:16, 0:2048], T.KDl[:, 0:128], ["KDl"], ["KW0"], "kw0", kb=32)
+    DMA(T.KW[1:128:16, 0:2048], T.KDh[:, 0:128], ["KDh"], ["KW1"], "kw1", "s", kb=32)
+    DMA(T.KW[2:128:16, 0:2048], T.KDl[:, 128:256], ["KDl"], ["KW2"], "kw2", kb=32)
+    DMA(T.KW[3:128:16, 0:2048], T.KDh[:, 128:256], ["KDh"], ["KW3"], "kw3", "s", kb=32)
+    KWK, KTK = ["KW0", "KW1", "KW2", "KW3"], ["KT0", "KT1", "KT2", "KT3"]
+    DMA(T.ZW[:, 0:2048], T.z[:], ["KDl", "KDh", "PDl", "PDh"], ["ZW"], "z", "y", 512, boost=-100.0)
+    DMA(T.RW[:, 0:2048], T.rs[:], ["KDl", "KDh", "PDl", "PDh"], ["RW"], "rs", "y", 512, boost=-200.0)
+    DMA(T.EW[:], T.env[:], ["KDl", "KDh", "PDl", "PDh"], ["EW"], "env", "y", 512, boost=-210.0)
+    DMA(T.OW[1:128:16, :], T.HIW[0:8, :], ["HIW", "KDh"], ["OW1"], "ow1", kb=40, boost=-220.0)
+    DMA(T.KW[0:128:16, 2048:MW], T.OW[0:128:16, 2048:MW], ["OW0"], ["KT0"], "kt0", kb=8, boost=-220.0)
+    DMA(T.KW[1:128:16, 2048:MW], T.HIW[0:8, 2048:MW], ["HIW"], ["KT1"], "kt1", kb=8, boost=-220.0)
+    DMA(T.KW[2:128:16, 2048:MW], T.OW[0:128:16, 2048:MW], ["OW0"], ["KT2"], "kt2", kb=8, boost=-220.0)
+    DMA(T.KW[3:128:16, 2048:MW], T.HIW[0:8, 2048:MW], ["HIW"], ["KT3"], "kt3", kb=8, boost=-220.0)
+
+    def wrap(bank, c0, wq, src, s0, n, R, W, nm):
+        PE(lambda e: [e.matmul(bank[:, c0:c0 + n], wq[:, 128 * q:128 * q + 128], src[:, s0 + q:s0 + 16 * n:16], q == 0, q == 15) for q in range(16)],
+           16 * max(64, n), R, W, nm)
+
+    def step(t, k, h, X, xk):
+        hs, win = str(h), (MW if t else 2048)
+        ck, tp, lp, tk = T["CK" + hs], T["bTP" + hs], T["bLP" + hs], "bTP" + hs
+        off, lk = LI(k, 64 * h, 64 * h + 64), ["L%d_%d" % (k, h)]
+        gather(ck[:, 0:HL], T.KW[:, 0:win], off, HL, lk + KWK + (KTK if t else []), ["CKk" + hs], "kid")
+        gatherop(ck[:, HL:2 * HL], T.ZW[:, 0:win], off, X[:, HL * h:HL * h + HL], A.is_le, lk + ["ZW", xk] + (["ZT"] if t else []), ["CKz" + hs], "z")
+        PE(lambda e: [e.matmul(tp[:, q:512:16], ck[:, q:2 * HL:16], T.RHS[:], True, True) for q in range(16)], 1024, ["CKk" + hs, "CKz" + hs] + RH, [tk], "T")
+        ma, mb_, ft = T["MA" + hs], T["MB" + hs], T["FT" + hs]
+        if MS[t][h]:
+            act(ma[:], tp[64:128, 0:128], F.Sign, ["c85"], ["MA" + hs, tk], "m", bias=T.COL[0:64, C["c85"]:C["c85"] + 1])
+        else:
+            vts(ma[:], tp[64:128, 0:128], 8.5, 0.5, A.is_ge, A.subtract, [], ["MA" + hs, tk], "m")
+        dc = 256 if MS[t][h] else 384
+        vtt(mb_[:], ma[:], tp[0:64, dc:dc + 128], A.mult, ["MA" + hs, tk], ["MB" + hs], "t", two=False)
+        vtt(ft[:], mb_[:], tp[0:64, 128:256], A.add, ["MB" + hs, tk], ["FT" + hs], "f", two=False)
+        PE(lambda e: e.matmul(lp[:, 0:64], ft[:, 0:128], T.IDF[0:64, 0:64], True, True), 256, ["FT" + hs, "IDF"], ["bLP" + hs], "tr")
+        vcopy(LI(k + 1, 64 * h, 64 * h + 64), lp[:, 0:64], [], ["L%d_%d" % (k + 1, h), "bLP" + hs], "list")
+
+    def outcome(t, X, xk):
+        win = MW if t else 2048
+        for h in range(2):
+            wrap(T["bOP%d" % h], 0, T.WQW, X, HL * h, 64, ["WQW", xk[h]], ["bOP%d" % h], "wc")
+        for h in range(2):
+            hs = str(h)
+            bo, cr, ss, mm = T["bOP" + hs], T["CR" + hs], T["SS" + hs], T["MM" + hs]
+            xh, a97 = X[:, HL * h:HL * h + HL], T.A97[:, 64 * h:64 * h + 64]
+            gatherop(cr[:], T.RW[:, 0:win], LI(4, 64 * h, 64 * h + 64), xh, A.is_gt, ["L4_%d" % h, "RW", xk[h]] + (["RTa", "RTb"] if t else []), ["CR" + hs], "R")
+            wrap(bo, 128, T.WQ1, cr, 0, 64, ["WQ1", "CR" + hs], ["bOP" + hs], "a")
+            i1, i2, ix = T.IT[:, 64 * h:64 * h + 64], T.IT[:, 128 + 64 * h:192 + 64 * h], LI(10, 64 * h, 64 * h + 64)
+            act(a97, bo[:, 128:192], F.Copy, [], ["A97" + hs, "bOP" + hs], "a97", scale=97.0)
+            vtt(i1, a97, bo[:, 0:64], A.add, ["A97" + hs], ["XI1" + hs, "bOP" + hs], "i1", two=False)
+            vts(i2, i1, 2047, None, A.bitwise_and, None, ["XI1" + hs], ["XI2" + hs], "i2")
+            vcopy(ix, i2, ["XI2" + hs], ["IX" + hs], "ix")
+            gatherop(ss[:], T.EW[:], ix, xh, A.add, ["IX" + hs, "EW", xk[h]], ["SS" + hs], "env")
+            vts(mm[:], ss[:], 0.0, 256.0, A.is_lt, A.mult, ["SS" + hs], ["MM" + hs], "mm", half=True)
+
+    def send(srcs, out, dst, rs, ls, R, W, nm, kb):
+        rid, pid = topo.addr(dst)[0], topo.addr(dst)[1]
+        k = dict(dst_ids=[DstId(rid=rid, pnc=pid)], dma_engine_mask=topo.mask(core, dst), remote_sem=T.sem[rs])
+        tr = RemoteDMATransfer(srcs=srcs, dsts=[out], alu_op=1, **k) if len(srcs) > 1 else RemoteDMATransfer(src=srcs[0], dst=out, **k)
+        op([("gr", 1.0, lambda e: e.remote_dma_fused([tr], local_sem=T.sem[ls]))], R, [nm], nm, lat=kb / 60.0, tok=(ls, len(topo.engines(core, dst))))
+        op([("arr", 0.0, None)], [nm], W, nm + "arr", lat=2.5, tok=(rs, len(topo.engines(prv if dst == nxt else nxt, core))))
+
+    def splits(t):
+        win, off = (MW if t else 2048), LI(4, 0, 16)
+        gather(T.OQ[:], T.OW[:, 0:win], off, S, ["L4_0", "OW0", "OW1"], ["OQ"], "oq")
+        gather(T.KQ[:], T.KW[:, 0:win], off, S, ["L4_0"] + KWK + (KTK if t else []), ["KQ"], "kq")
+        gather(T.RF[:], T.RW[:, 0:win], off, S, ["L4_0", "RW"] + (["RTa", "RTb"] if t else []), ["RF"], "rf")
+        PE(lambda e: [e.matmul(T.bMI[:, 0:256], T.OB[:], T.OQ[:], True, True)], 256, ["OB", "OQ"], ["bMI"], "FR")
+        PE(lambda e: [e.matmul(T.bLP0[:, 256:512], T.OB[:], T.KQ[:], True, False),
+                      e.matmul(T.bLP0[:, 256:512], T.OBN[:], T.OQ[:], False, True)], 512, ["OB", "OBN", "OQ", "KQ"], ["bLP0"], "LD")
+        vts(T.FI[:], T.bMI[:, 0:256], col("sc"), None, A.mult, None, ["sc"], ["FI", "bMI"], "fi")
+        vts(T.LF[:], T.bLP0[:, 256:512], 0.0, None, A.is_equal, None, [], ["LF", "bLP0"], "lf")
+        vts(T.FB[:], T.FI[:], 2048, None, A.bitwise_and, None, ["FI"], ["FB"], "fb")
+        vts(T.FBI[:], T.FB[:], 1.0 / 1024, -1.0, A.mult, A.add, ["FB"], ["FBI"], "fbi")
+        for fx, c in (("FE", "me"), ("FO", "mo")):
+            op([("s", 0.28, lambda e, fx=fx, c=c: e.activation(T[fx][:], T.FBI[:], F.Copy, scale=col(c))),
+                ("v", 0.16, lambda e, fx=fx, c=c: e.tensor_scalar(T[fx][:], T.FBI[:], col(c), None, A.mult))], ["FBI", c], [fx], "fx")
+        for gr in range(8):
+            p0, fk, bn = 32 * (gr // 2), "FO" if gr % 2 else "FE", ("bTP1", "bSP", "bTP0", "bMI")[gr % 4]
+
+            def fn(e, p0=p0, fk=fk, bn=bn):
+                r, bk, fx, fb = [], T[bn], T[fk], T.FBI
+                r.append(e.matmul(bk[:, 0:128], fx[p0:p0 + 32, 0:128], fb[p0:p0 + 32, 0:128], True, False))
+                r.append(e.matmul(bk[:, 0:128], T.IDB[:], T.MASK[:], False, True))
+                r.append(e.matmul(bk[:, 128:256], fx[p0:p0 + 32, 128:256], fb[p0:p0 + 32, 0:128], True, True))
+                r.append(e.matmul(bk[:, 256:384], fx[p0:p0 + 32, 128:256], fb[p0:p0 + 32, 128:256], True, False))
+                r.append(e.matmul(bk[:, 256:384], T.IDB[:], T.MASK[:], False, True))
+                return r
+            PE(fn, 640, [fk, "FBI", "IDB", "MASK"], [bn], "dot")
+
+            def fs(e, bn=bn, gr=gr):
+                return [e.activation(T.JK[:, 512 * (gr % 2) + a:512 * (gr % 2) + b], T[bn][:, a:b], F.Relu, accum_out=T.DM[:, 8 * hf + gr:8 * hf + gr + 1]) for hf, a, b in ((0, 0, 128), (1, 128, 384))]
+
+            def fv(e, bn=bn, gr=gr):
+                return [e.tensor_reduce(T.DM[:, 8 * hf + gr:8 * hf + gr + 1], T[bn][:, a:b], AxisListType.X, A.max) for hf, a, b in ((0, 0, 128), (1, 128, 384))]
+            op([("s", 0.5, fs), ("v", 0.42, fv)], [], ["JK%d" % (gr % 2), "DM%d" % gr, bn], "red")
+        vts(T.DUP[:], T.DM[:], 0.5, None, A.is_ge, None, ["DM%d" % b for b in range(8)], ["DUP"], "dup")
+        PE(lambda e: e.matmul(T.bLP1[0:16, 0:128], T.DUP[:], T.IDB[:], True, True), 128, ["DUP", "IDB"], ["bLP1"], "dupT")
+        op([("s", 0.17, lambda e: e.activation(T.DUT[:], T.bLP1[0:16, 0:128], F.Copy)), ("v", 0.16, lambda e: e.tensor_copy(T.DUT[:], T.bLP1[0:16, 0:128]))], [], ["DUT", "bLP1"], "dut")
+        PE(lambda e: [e.matmul(T.bSP[:, 0:256], a_[:], b_, i_ == 0, i_ == 2) for i_, (a_, b_) in enumerate(((T.IDB, T.RF[:]), (T.IDN, T.SS0[:, 0:S]), (T.IDN, T.MM0[:, 0:S])))] +
+           [e.matmul(T.bSP[:, 256:512], T.IDB[:], b_, i_ == 0, i_ == 2) for i_, b_ in enumerate((T.RF[:], T.SS0[:, 0:S], T.MM0[:, 0:S]))],
+           1536, ["IDB", "IDN", "RF", "SS0", "MM0"], ["bSP"], "rv")
+        act(T.AD[:], T.bSP[:, 0:256], F.Abs, [], ["AD", "bSP"], "abs")
+        vcopy(T.RS1[:], T.bSP[:, 256:512], [], ["RS1", "bSP"], "rs1")
+
+        def fn3(e):
+            r = []
+            for hh in range(2):
+                o, sl = T.bMI[:, 128 * hh:128 * hh + 128], slice(128 * hh, 128 * hh + 128)
+                r.append(e.matmul(o, T.BLK[:], T.AD[:, sl], True, False))
+                r.append(e.matmul(o, T.I8K[:], T.LF[:, sl], False, False))
+                r.append(e.matmul(o, T.EH[:, sl], T.DUT[:], False, True))
+            return r
+        PE(fn3, 768, ["BLK", "AD", "I8K", "LF", "EH", "DUT"], ["bMI"], "far")
+        vts(T.SP[:], T.bMI[:, 0:256], T.THC[:], None, A.is_ge, None, ["THC"], ["SP", "bMI"], "sp")
+        RN, rn, c0 = (T.YR1, "YR1", 0) if t else (T.RW, "RT", 2048)
+        vts(T.RS2[:], T.RS1[:], 1, None, A.arith_shift_right, None, ["RS1"], ["RS2"], "rs2")
+        vtt(RN[:, c0:c0 + 512:2], T.RF[:], T.SP[:], A.mult, ["RF", "SP"], [rn + "a"], "rna")
+        vtt(RN[:, c0 + 1:c0 + 512:2], T.RS2[:], T.SP[:], A.mult, ["RS2", "SP"], [rn + "b"], "rnb")
+        wrap(T.bSP, 0, T.WQP, T.SP, 0, 16, ["SP", "WQP"], ["bSP"], "wsp")
+        vcopy(T.TG[:, 0:16], LI(4, 0, 16), ["L4_0"], ["TG0"])
+        vtt(T.TG[:, 16:32], T.TG[:, 0:16], T.DW[:], A.subtract, ["TG0", "DW"], ["TG1"])
+        vts(T.TG[:, 32:48], T.bSP[:, 0:16], 1.0, None, A.is_ge, None, [], ["TG2", "bSP"])
+        vtt(T.TG[:, 48:64], T.TG[:, 16:32], T.TG[:, 32:48], A.mult, ["TG1", "TG2"], ["TG3"])
+        vtt(T.TG[:, 64:80], T.TG[:, 48:64], T.DW[:], A.add, ["TG3", "DW"], ["TG4"])
+        vcopy(LI(11, 0, 16), T.TG[:, 64:80], ["TG4"], ["TGL"])
+
+        def scat(win_, val, R, W, nm):
+            op([("v", 0.05 + S * 3.5 * CYC, lambda e: e.tensor_copy(win_.indirect(LI(11, 0, 16)), val))], R + ["TGL"], W, nm)
+        if not t:
+            scat(T.KW[:], T.NK[:], ["NK"], KWK + KTK, "scK")
+            scat(T.ZW[:], T.XF[:], ["XF"], ["ZW", "ZT"], "scZ")
+        scat(T.KF[:], (T.NV1 if t else T.NV0)[:], ["NV1" if t else "NV0"], ["KF0", "KF1", "KFt"], "scF")
+
+    for k in range(4):
+        for h in range(2):
+            gather(T["XS%d" % k][:, HL * h:HL * h + HL], T.XW[:], LI(5 + k, 64 * h, 64 * h + 64), HL, ["XW", "SL%d_%d" % (k, h)], ["XS%d_%d" % (k, h)], "xs")
+        for h in range(2):
+            if k < 3:
+                gather(T["PT%d" % h][:], T.PW[:], LI(5 + k, 64 * h, 64 * h + 64), HL, ["PW0", "PW1", "SL%d_%d" % (k, h)], ["PT%d" % h], "pv")
+                wrap(T.bSP, 0, T.WQP, T["PT%d" % h], 0, 64, ["WQP", "PT%d" % h], ["bSP"], "ws")
+                vcopy(LI(6 + k, 64 * h, 64 * h + 64), T.bSP[:, 0:64], [], ["SL%d_%d" % (k + 1, h), "bSP"], "slist")
+        for h in range(2):
+            step(0, k, h, T["XS%d" % k], "XS%d_%d" % (k, h))
+    gather(T.PT2[:], T.PW[:], LI(8, 0, 16), S, ["PW0", "PW1", "SL3_0"], ["PT2"], "p4")
+    wrap(T.bSP, 0, T.WQP, T.PT2, 0, 16, ["WQP", "PT2"], ["bSP"], "ws4")
+    vcopy(T.SW[:, 64:80], T.bSP[:, 0:16], [], ["SW4", "bSP"])
+    for k in range(5):
+        vcopy(T.FW[:, 16 * k:16 * k + 16], LI(k, 0, 16), ["L%d_0" % k], ["FW%d" % k])
+        if k < 4:
+            vcopy(T.SW[:, 16 * k:16 * k + 16], LI(5 + k, 0, 16), ["SL%d_0" % k], ["SW%d" % k])
+    vtt(T.SFa[:], T.FW[:, 16:80], T.FW[:, 0:64], A.not_equal, ["FW%d" % k for k in range(5)], ["SFa"])
+    vtt(T.SFb[:], T.SW[:, 16:80], T.SW[:, 0:64], A.subtract, ["SW%d" % k for k in range(5)], ["SFb"])
+    vtt(T.SFa[:], T.SFa[:], T.SFb[:], A.mult, ["SFa", "SFb"], ["SFa"])
+    vtt(T.SFb[:, 0:32], T.SFa[:, 0:32], T.SFa[:, 32:64], A.add, ["SFa"], ["SFb"])
+    vtt(T.SFa[:, 0:16], T.SFb[:, 0:16], T.SFb[:, 16:32], A.add, ["SFb"], ["SFa"])
+    vtt(T.SFb[:, 32:48], T.SFa[:, 0:16], T.SW[:, 0:16], A.add, ["SFa", "SW0"], ["SFb"])
+    vcopy(LI(11, 32, 48), T.SFb[:, 32:48], ["SFb"], ["SFL"])
+    gather(T.XF[:], T.XW[:], LI(11, 32, 48), S, ["XW", "SFL"], ["XF"], "xf")
+
+    act(T.EW[:], T.EW[:], F.Copy, ["EW"], ["EW"], "env256", bias=-256.0)
+    outcome(0, T.XS0, ["XS0_0", "XS0_1"])
+    for h in range(2):
+        hs = str(h)
+        send([T["SS" + hs][:], T["MM" + hs][:]], T.VL[:, HL * h:HL * h + HL], nxt, "aA" + hs, "lA" + hs, ["SS" + hs, "MM" + hs], ["VL%d" % h], "send" + hs, 256)
+    vcopy(T.thF[:], T.thI[:], ["thI"], ["thF"])
+    PE(lambda e: e.matmul(T.bMI[:, 0:1], T.E8[:], T.thF[:], True, True), 256, ["E8", "thF"], ["bMI"], "th")
+    vts(T.THC[:], T.bMI[:, 0:1], BIG, None, A.add, None, [], ["THC", "bMI"])
+    vcopy(T.KDf[:], T.KD[:], ["KD0", "KD1"], ["KDf"])
+    DMA(T.KF[0:128:16, 0:2048], T.KDf[:, 0:128], ["KDf"], ["KF0"], "kf0", boost=-30.0)
+    DMA(T.KF[1:128:16, 0:2048], T.KDf[:, 128:256], ["KDf"], ["KF1"], "kf1", boost=-30.0)
+    splits(0)
+    DMA(T.yr[:, 0:512], T.RW[:, 2048:MW], ["RTa", "RTb"], ["oyr0"], "oyr0")
+    vcopy(T.cuF[:], T.cuI[:], ["cuI"], ["cuF"])
+    PE(lambda e: e.matmul(T.bLP1[:, 0:128], T.cuF[:], T.IDF[:], True, True), 512, ["cuF", "IDF"], ["bLP1"], "cuT")
+    vcopy(T.cuT[:], T.bLP1[:, 0:128], [], ["cuT", "bLP1"])
+    for gr in range(8):
+        DMA(T.CF[16 * gr:16 * gr + 1, :], T.cuT[:, 16 * gr:16 * gr + 16], ["cuT", "CF"], ["CF%d" % gr], "cf", kb=8)
+    send([T.wI[:]], T.wN[:], prv, "aw", "lw", ["wI"], ["wN"], "sendw", 1)
+    vcopy(col("wn"), T.wN[:], ["wN"], ["wn"])
+    act(T.WQN[:], T.WQ1[:], F.Copy, ["WQ1", "wn"], ["WQN"], "WQN", scale=col("wn"))
+
+    for h in range(2):
+        hs = str(h)
+        wrap(T["bOP" + hs], 64, T.WQW, T.VL, HL * h, 64, ["WQW", "VL%d" % h], ["bOP" + hs], "wh")
+        i1, i2 = T.IT[:, 256 + 64 * h:320 + 64 * h], T.IT[:, 384 + 64 * h:448 + 64 * h]
+        vcopy(i1, T["bOP" + hs][:, 64:128], [], ["HI1" + hs, "bOP" + hs], "h1")
+        vts(i2, i1, 2047, None, A.bitwise_and, None, ["HI1" + hs], ["HI2" + hs], "h2")
+        vcopy(LI(9, 64 * h, 64 * h + 64), i2, ["HI2" + hs], ["LH" + hs], "h3")
+    for k in range(4):
+        for h in range(2):
+            if k:
+                gather(T["YS%d" % k][:, HL * h:HL * h + HL], T["XS%d" % (k - 1)][:], LI(9, 64 * h, 64 * h + 64), HL, ["XS%d_0" % (k - 1), "XS%d_1" % (k - 1), "LH%d" % h], ["YS%d_%d" % (k, h)], "ys")
+        for h in range(2):
+            step(1, k, h, T["YS%d" % k] if k else T.VL, "YS%d_%d" % (k, h) if k else "VL%d" % h)
+    for h in range(2):
+        gather(T.HG[:, HL * h:HL * h + HL], T.CF[:], LI(9, 64 * h, 64 * h + 64), HL, ["CF"] + ["CF%d" % a for a in range(8)] + ["LH%d" % h], ["HG%d" % h], "cur")
+        DMA(T.yp[:, HL * h:HL * h + HL], T.HG[0:128:16, HL * h:HL * h + HL], ["HG%d" % h], ["oyp%d" % h], "oyp", kb=32)
+    outcome(1, T.VL, ["VL0", "VL1"])
+
+    def fnh(h):
+        def fn(e):
+            r = []
+            for j in range(8):
+                for src in (T["SS%d" % h], T["MM%d" % h]):
+                    q = 128 * (8 * h + j)
+                    r.append(e.matmul(T.bOP0[:, 192:320], T.WQN[:, q:q + 128], src[:, 128 * j:128 * j + 128], h == 0 and not r, h == 1 and len(r) == 15))
+            return r
+        return fn
+    for h in range(2):
+        PE(fnh(h), 2048, ["WQN", "SS%d" % h, "MM%d" % h], ["bOP0"], "hd")
+    i1, i2 = T.IT[:, 256:384], T.IT[:, 384:512]
+    vcopy(i1, T.bOP0[:, 192:320], [], ["HI10", "HI11", "bOP0"], "H1")
+    vts(i2, i1, 2047, None, A.bitwise_and, None, ["HI10", "HI11"], ["HI20", "HI21"], "H2")
+    vts(T.HS[:], i2, 4096.0, None, A.add, None, ["HI20", "HI21"], ["HS"], "H3")
+    send([T.HS[:]], T.HR[:], nxt, "aH", "lH", ["HS"], ["HR"], "sendH", 64)
+    DMA(T.yp[:, 2048:4096], T.HR[:], ["HR"], ["oyp2"], "oyp2")
+    splits(1)
+    DMA(T.yr[:, 512:1024], T.YR1[:], ["YR1a", "YR1b"], ["oyr1"], "oyr1", kb=128)
+    DMA(T.yk0[:], T.KF[0:128:16, 0:3072], ["KF0", "KFt"], ["oyk0"], "oyk0", kb=96)
+    DMA(T.yk1[:], T.KF[1:128:16, 0:3072], ["KF1", "KFt"], ["oyk1"], "oyk1", "s", kb=96)
+
+    if "order" not in PLANS:
+        PLANS["order"], PLANS["score"] = make_plan(ops)
+    eng = {"v": g.vector, "s": g.scalar, "t": g.tensor, "g": g, "y": g.sync}
+    cs = {"v": "cv", "s": "cs", "t": "ct", "g": "cg"}
+    cnt = dict((s_, 0) for s_ in cs.values())
+    known = dict((q, {}) for q in eng)
+    total, token = {}, [None] * len(ops)
+    for i, j in PLANS["order"]:
+        q, d, fn = ops[i]["alts"][j]
+        if q == "arr":
+            s_, v = ops[i]["tok"]
+            token[i] = (s_, v, {s_: v})
+            total[s_] = v
+            continue
+        r = q[0]
+        kn, e = known[r], eng[r]
+        need = {}
+        for dp in ops[i]["deps"]:
+            s_, v, ck = token[dp]
+            if kn.get(s_, 0) < v and need.get(s_, (0, None))[0] < v:
+                need[s_] = (v, ck)
+        for s_ in sorted(need, key=lambda s_: (-len(need[s_][1]), s_)):
+            v, ck = need[s_]
+            if kn.get(s_, 0) >= v:
+                continue
+            e.wait_ge(T.sem[s_], v)
+            for a, b in ck.items():
+                if kn.get(a, 0) < b:
+                    kn[a] = b
+        out = fn(e)
+        if q in cs:
+            for x in (out if isinstance(out, list) else [out]):
+                x.then_inc(T.sem[cs[q]], 1)
+                cnt[cs[q]] += 1
+            s_, v = cs[q], cnt[cs[q]]
+        else:
+            s_, v = ops[i]["tok"]
+        total[s_] = v
+        ck = dict(kn)
+        ck[s_] = v
+        token[i] = (s_, v, ck)
+    for s_ in sorted(total):
+        if known["g"].get(s_, 0) < total[s_]:
+            g.wait_ge(T.sem[s_], total[s_])

@@ -1,5 +1,5 @@
 from concourse.bass import DstId, RemoteDMATransfer
-from concourse.mybir import AluOpType as A, ActivationFunctionType as F, AxisListType
+from concourse.mybir import AluOpType as A, ActivationFunctionType as F
 
 S, HL = 256, 1024
 MW = 2560
@@ -19,21 +19,20 @@ def _decl(where, dtype, text):
 
 
 _decl("sbuf", BFB, "XW:4096 PW:4096 ZW:3328 KW:3328 RW:2560 EW:2048 OW:2560 HIW:2560 VL:2048 KDl:256 KDh:256 PDl:256 PDh:256 ONB:128 ZB:256 "
-      "IDB:128 IDN:128 I8K:128 BC8:8 SEL:128 BLK:128 MASK:128 EH:16x256 RHS:32 RT:32 OB:128 OBN:128 WQ1:2048 WQP:2048 WQW:2048 WQN:2048 LOI:256 "
+      "IDB:128 I8K:128 BC8:8 BLK:128 I4B:256 BASE:256 DR:256 WN8:8 EH:16x256 RHS:24 RT:8 OB:128 OBN:128 WQ1:2048 WQP:2048 WQW:2048 LOI:256 "
       "HII:256 NK:256 NKb:256 YR1:512 XF:256 PT2:256 RF:256 KQ:256 OQ:256 FBI:256 FE:256 FO:256 LF:256 DUP:16 DUT:16x128 JK:1024 AD:256 SP:256 "
       "XS0:2048 XS1:2048 XS2:2048 XS3:2048 YS1:2048 YS2:2048 YS3:2048 CK0:2048 CK1:2048 CR0:1024 CR1:1024 PT0:1024 PT1:1024 SS0:1024 SS1:1024 MM0:1024 MM1:1024")
-_decl("sbuf", FP, "KF:3328 CF:2048 HG:2048 thF:8x1 THC:1 KDf:256 cuF:128 cuT:128 ONF:128 IDF:128 E8:8x128 COL:64 DW:16 NV0:256 NV1:256 FW:80 SW:80 "
-      "SFa:64 SFb:64 HR:128 HS:128 DM:16 TG:80 A97:128 MA0:64x128 MA1:64x128 MB0:64x128 MB1:64x128 FT0:64x128 FT1:64x128")
-_decl("sbuf", I4, "stI:128 cuI:128 KD:256 PD:256 wI:1 wN:1 thI:8x1 KDt:256 KDu:256 PDt:256 PDu:256 KI:1 CI:16 FI:256 FB:256 RS1:256 RS2:256 IT:512")
+_decl("sbuf", FP, "KF:3328 CF:2048 HG:2048 thF:8x1 THC:1 KDf:256 cuF:128 cuT:128 ONF:128 IDF:128 E8:8x128 COL:32 CT:32x16 EQ:16x128 EQ2:32x128 DW:16 NV0:256 "
+      "NV1:256 FW:80 SW:80 SFa:64 SFb:64 HR:128 HS:128 HFT:128 DM:16 TG:80 A97:128 MA0:64x128 MA1:64x128 MB0:64x128 MB1:64x128 FT0:64x128 FT1:64x128")
+_decl("sbuf", I4, "stI:128 cuI:128 KD:256 PD:256 wI:1 wN:1 thI:8x1 KDt:256 KDu:256 PDt:256 PDu:256 FI:256 FB:256 RS1:256 RS2:256 IT:512")
 _decl("sbuf", U2, "LL:1536")
 _decl("psum", FP, "bMI:512 bSP:512 bTP0:512 bTP1:512 bLP0:512 bLP1:512 bOP0:512 bOP1:512")
 SEMAPHORES = ["cv", "cs", "ct", "cg"] + ["d%d" % _k for _k in range(48)] + ["aw", "lw", "aA0", "aA1", "lA0", "lA1", "aH", "lH"]
 
 CYC, GAT = 0.83e-3, 1.56
 WAKE, SELF, DBW, DLAT = 0.12, 0.08, 250.0, 2.0
-MS = ((1, 0), (0, 0))
-ONLY = {"ki": "s", "xs": "s", "pv": "v", "ys": "b", "cu": "s"}
-BETA, TRIES = 0.03, 400
+PREF = {"ki": 0, "xs": 0, "pv": 1, "ys": 0, "cu": 0}
+BETA, TRIES, PCF, SEED0 = 0.03, 6000, 1.15, 7
 MODELS = ((1.2, 1.0, 0.12, 1.0, 1.0), (1.2, 0.72, 0.25, 1.5, 1.3), (1.3, 1.25, 0.1, 0.8, 1.0))
 PLANS = {}
 
@@ -68,7 +67,7 @@ def make_plan(ops):
                         best = (key, i, j, st)
             _, i, j, st = best
             open_.remove(i)
-            q, d = rq[i][j], ops[i]["alts"][j][1]
+            q, d = rq[i][j], ops[i]["alts"][j][1] * (PCF if rq[i][j] in "vstg" else 1.0)
             if q != "arr":
                 free[q] = st + d
             fin = st + d + ops[i]["lat"]
@@ -83,19 +82,23 @@ def make_plan(ops):
                     open_.append(s_)
         return order
 
-    def score(order):
-        tot = 0.0
-        for cf, gf, wk, bf, lf in MODELS:
-            fin, free, bw, mx = [0.0] * n, {}, 0.0, 0.0
+    def score(order, watch):
+        tot, way = 0.0, []
+        for mi, (cf, gf, wk, bf, lf) in enumerate(MODELS):
+            fin, free, bw, mx, end = [0.0] * n, {}, 0.0, 0.0, 0
+            prev, why = {}, [None] * n
             for i, j in order:
                 o, q = ops[i], rq[i][j]
                 d = o["alts"][j][1]
                 if q in "vstg" and not dma[i]:
                     d *= cf * (gf if o["gat"] else 1.0)
                 t = 0.0 if q == "arr" else free.get(q, 0.0)
+                w = (prev.get(q), True)
                 for x in o["deps"]:
                     if fin[x] + wk > t:
                         t = fin[x] + wk
+                        w = (x, False)
+                why[i], prev[q] = w, i
                 e = t + d
                 if q != "arr":
                     free[q] = e
@@ -105,30 +108,43 @@ def make_plan(ops):
                 else:
                     e += o["lat"] * lf
                 fin[i] = e
-                mx = max(mx, e)
+                if e > mx:
+                    mx, end = e, i
             tot += mx / (cf * (1 + gf))
-        return tot
-    boost, pick = [o["boost"] for o in ops], [-1] * n
+            if mi == watch:
+                x = end
+                while x is not None:
+                    way.append((x, why[x][0] if why[x][1] else None))
+                    x = why[x][0]
+        return tot, way
+    boost, pick = [o["boost"] for o in ops], [o["pref"] for o in ops]
     two = [i for i in range(n) if len(rq[i]) == 2]
     order = schedule(boost, pick, BETA)
-    best, seed = score(order), [7]
+    seed = [SEED0]
+    best, way = score(order, 0)
 
     def rnd():
         seed[0] = (seed[0] * 1103515245 + 12345) % 2147483648
         return seed[0] / 2147483648.0
     for it in range(TRIES):
         b2, p2 = list(boost), list(pick)
-        share, amp = 0.02 + 0.3 * rnd() ** 2, 2.0 + 12.0 * rnd()
-        for i in range(n):
-            if rnd() < share:
-                b2[i] += amp * (2 * rnd() - 1)
-        for i in two:
-            if rnd() < share:
-                p2[i] = int(3 * rnd()) - 1
+        share, amp = 0.02 + 0.4 * rnd() ** 2, 1.0 + 12.0 * rnd()
+        for i, before in way:
+            if before is not None and rnd() < share:
+                b2[i] += amp * rnd()
+                b2[before] -= amp * rnd()
+        if rnd() < 0.5:
+            for i in two:
+                if rnd() < 0.04:
+                    p2[i] = int(3 * rnd()) - 1
+        if rnd() < 0.3:
+            for i in range(n):
+                if rnd() < 0.04:
+                    b2[i] += amp * (2 * rnd() - 1)
         o2 = schedule(b2, p2, BETA)
-        s2 = score(o2)
+        s2, w2 = score(o2, int(rnd() * len(MODELS)))
         if s2 <= best:
-            best, order, boost, pick = s2, o2, b2, p2
+            best, order, boost, pick, way = s2, o2, b2, p2, w2
     return order, best
 
 
@@ -138,12 +154,12 @@ def rank_program(g, core, T, topo):
         return
     n_ranks = len(T.cores)
     nxt, prv = T.cores[(rank + 1) % n_ranks], T.cores[(rank - 1) % n_ranks]
-    ops, last, readers = [], {}, {}
+    ops, last, readers, fore = [], {}, {}, [0.0]
 
     def LI(k, a, b):
         return T.LL[:, 128 * k + a:128 * k + b]
 
-    def op(alts, R, W, nm="", lat=0.0, tok=None, boost=0.0, gat=False):
+    def op(alts, R, W, nm="", lat=0.0, tok=None, boost=0.0, gat=False, pref=-1):
         i, deps = len(ops), set()
         for k in list(R) + list(W):
             if k in last:
@@ -156,7 +172,7 @@ def rank_program(g, core, T, topo):
             last[k] = i
             readers[k] = []
         deps.discard(i)
-        ops.append(dict(alts=alts, deps=deps, nm=nm, lat=lat, tok=tok, boost=boost, gat=gat))
+        ops.append(dict(alts=alts, deps=deps, nm=nm, lat=lat, tok=tok, boost=boost + (fore[0] if alts[0][0] in "vstg" else 0.0), gat=gat, pref=pref))
 
     def vc(n, half=False):
         return 0.05 + max(64, n * (0.5 if half else 1)) * CYC
@@ -189,8 +205,7 @@ def rank_program(g, core, T, topo):
         d = n * GAT * CYC
         a = [("s", 0.07 + d, lambda e: e.activation(out, win.indirect(off), F.Copy)),
              ("v", 0.06 + d, lambda e: e.tensor_copy(out, win.indirect(off)))]
-        o_ = ONLY.get(nm[:2], "b")
-        op(a[:1] if o_ == "s" else a[1:] if o_ == "v" else a, R, W, nm, gat=True)
+        op(a, R, W, nm, gat=True, pref=PREF.get(nm[:2], -1))
 
     def gatherop(out, win, off, in1, o, R, W, nm):
         op([("v", 0.06 + HL * GAT * CYC, lambda e: e.tensor_tensor(out, win.indirect(off), in1, o))], R, W, nm, gat=True)
@@ -207,105 +222,123 @@ def rank_program(g, core, T, topo):
     def aff(out, in_, pat, cmpo, fill, base, cm, R, W):
         op([("g", cnt_(pat), lambda e: e.affine_select(out, in_, pat, cmpo, fill, base, cm))], R, W)
 
-    def iota(out, pat, base, cm, W):
-        op([("g", cnt_(pat), lambda e: e.iota(out, pat, base, cm, allow_small_or_imprecise_dtypes=True))], [], W)
+    def iota(out, pat, base, cm, W, R=()):
+        op([("g", cnt_(pat), lambda e: e.iota(out, pat, base, cm, allow_small_or_imprecise_dtypes=True))], R, W)
 
-    B = 90.0
+    B, KWK, KTK = 90.0, ["KW0", "KW1", "KW2", "KW3"], ["KT0", "KT1", "KT2", "KT3"]
     DMA(T.KD[:, 0:128], T.kid0[:], [], ["KD0"], "kid0", "y", boost=B)
     DMA(T.PD[:], T.prev[:], [], ["PD"], "prev", "s", 128, boost=B)
     DMA(T.KD[:, 128:256], T.kid1[:], [], ["KD1"], "kid1", "y", boost=B - 1)
     DMA(T.cuI[:], T.cur[:], [], ["cuI"], "cur", "s", boost=B - 1)
     DMA(T.stI[:], T.start[:], [], ["stI"], "start", "y", boost=B - 2)
-    DMA(T.XW[:], T.x[:], [], ["XW"], "x", "s", 1024, boost=B - 2)
+    DMA(T.XW[:], T.x[:], [], ["XW"], "x", "s", 1024, boost=B - 60)
+    DMA(T.ZW[:, 0:2048], T.z[:], [], ["ZW"], "z", "y", 512, boost=B - 70)
     DMA(T.wI[:], T.w[:], [], ["wI"], "w", "y", 1, boost=B - 3)
     DMA(T.thI[:], T.th[:], [], ["thI"], "th", "y", 1, boost=B - 7)
 
+    fore[0] = 80.0
     ms(T.ONB[:], 1.0, ["ONB"])
-    ms(T.PW[:], 0.0, ["PW0", "PW1"])
-    ms(T.ONF[:], 1.0, ["ONF"], half=False)
     ms(T.ZB[:], 0.0, ["ZB"])
+    ms(T.WQP[:], 0.0, ["WQP"])
+    fore[0] = 0.0
+    ms(T.PW[:], 0.0, ["PW0", "PW1"])
+    fore[0] = 60.0
+    act(T.KW[:, 0:2048], T.WQP[:], F.Copy, ["WQP"], KWK, "zero")
+    fore[0] = 0.0
+    ms(T.ONF[:], 1.0, ["ONF"], half=False)
     ms(T.ZW[:, 2048:MW], 0.0, ["ZT"])
-    aff(T.SEL[:], T.ONB[:], [[-1, 16], [-16, 8]], A.is_equal, 0.0, 0, 1, ["ONB"], ["SEL"])
+    fore[0] = 70.0
     aff(T.BC8[:], T.ONB[:, 0:8], [[-16, 8]], A.is_ge, 0.0, 0, 1, ["ONB"], ["BC8"])
     aff(T.BC8[:], T.BC8[:], [[16, 8]], A.is_ge, 0.0, 15, -1, ["BC8"], ["BC8"])
+    fore[0] = 0.0
     aff(T.IDF[:], T.ONF[:], [[-1, 128]], A.is_equal, 0.0, 0, 1, ["ONF"], ["IDF"])
-    op([("g", 0.2, lambda e: e.iota(T.KI[:], [[0, 1]], 0, 1))], [], ["KI"])
     aff(T.BLK[:], T.ONB[:], [[-16, 8], [0, 16]], A.is_ge, 0.0, 0, 1, ["ONB"], ["BLK"])
     aff(T.BLK[:], T.BLK[:], [[16, 8], [0, 16]], A.is_ge, 0.0, 15, -1, ["BLK"], ["BLK"])
-    iota(T.WQP[:], [[0, 2048]], 0, 0, ["WQP"])
-    iota(T.WQ1[:], [[0, 2048]], 0, 0, ["WQ1"])
+    iota(T.KW[:, 2048:MW], [[0, MW - 2048]], 0, 0, KTK)
+    fore[0] = -60.0
     iota(T.OW[:], [[0, 10], [1, 256]], 0, 0, ["OW0", "OW1"])
     iota(T.HIW[:], [[1, 10], [0, 256]], 0, 0, ["HIW"])
-    aff(T.MASK[:], T.ZB[:, 0:128], [[-1, 128]], A.is_gt, -8.0, 0, 1, ["ZB"], ["MASK"])
+    fore[0] = 0.0
+    iota(T.I4B[:], [[4, 256]], 0, 0, ["I4B"])
     aff(T.EH[:], T.ZB[0:16, :], [[-8, 2], [-1, 8], [0, 16]], A.not_equal, -BIG, 0, 1, ["ZB"], ["EH"])
     aff(T.E8[:], T.ONF[0:8, :], [[-1, 8], [0, 16]], A.is_equal, 0.0, 0, 1, ["ONF"], ["E8"])
     iota(T.DW[:], [[16, 16]], DUMP, 0, ["DW"])
     iota(T.NV0[:], [[2, 256]], 2048, 0, ["NV0"])
     iota(T.LOI[:], [[0, 2], [2, 128]], 0, 0, ["LOI"])
     iota(T.HII[:], [[1, 2], [0, 128]], 8, 0, ["HII"])
+    fore[0] = -60.0
     iota(T.KF[:, 2048:3072], [[1, 1024]], 2048, 0, ["KFt"])
     iota(T.CF[:], [[0, 2048]], 0, 0, ["CF"])
-    act(T.KW[:, 0:MW], T.PW[:, 0:MW], F.Copy, ["PW0", "PW1"], ["KW0", "KW1", "KW2", "KW3", "KT0", "KT1", "KT2", "KT3"], "kwz")
 
-    C = {}
+    TAB = {"k": (), "e1": ((1, 1),), "e2": ((2, 1),), "e02": ((0, 1), (2, 1)), "e13": ((1, 1), (3, 1)), "pc": ((0, 1), (1, 256)),
+           "pn": ((0, -1), (1, -256)), "sc": tuple((k, 2 ** (11 - k)) for k in range(12)), "e12": ((12, 1),), "c12": ()}
+    NT = len(TAB)
+    C = dict((nm, j) for j, nm in enumerate(list(TAB) + ["me", "mo", "q0b", "q1b", "p", "q0", "q1", "w", "wn"]))
 
     def col(nm):
-        C.setdefault(nm, len(C))
         return T.COL[:, C[nm]:C[nm] + 1]
+    fore[0] = 40.0
+    ms(T.CT[:], 0.0, ["CT" + nm for nm in C], half=False)
+    fore[0] = 0.0
+    for nm in TAB:
+        c, ck = T.CT[0:16, C[nm]:C[nm] + 1], ["CT" + nm]
+        if nm == "k":
+            iota(c, [[0, 1]], 0, 1, ck)
+        if nm == "c12":
+            aff(c, c, [[0, 1]], A.is_equal, -1024.0, -12, 1, ck, ck)
+        for k, v in TAB[nm]:
+            aff(c, c, [[0, 1]], A.not_equal, float(v), -k, 1, ck, ck)
+    u = 2.0 ** -20
+    for nm, o in (("me", 0), ("mo", 16)):
+        c, ck = T.CT[:, C[nm]:C[nm] + 1], ["CT" + nm]
+        aff(c, c, [[0, 1]], A.is_gt, u, 16 if o else -11, -1 if o else 1, ck, ck)
+        for k, v in ((12, -u), (13, -5.5 * u), (14, -5.5 * u)) + (((15, 0.0),) if o else ()):
+            aff(c, c, [[0, 1]], A.not_equal, v, -k - o, 1, ck, ck)
+    aff(T.EQ[:], T.ONF[0:16, :], [[0, 8], [1, 16]], A.is_equal, 0.0, 0, -1, ["ONF"], ["EQ"])
+    aff(T.EQ2[:], T.ONF[0:32, :], [[0, 4], [1, 32]], A.is_equal, 0.0, 0, -1, ["ONF"], ["EQ2"])
+    PE(lambda e: [e.matmul(T.bMI[:, 0:NT], T.EQ[:], T.CT[0:16, 0:NT], True, True), e.matmul(T.bMI[:, NT:NT + 2], T.EQ2[:], T.CT[:, NT:NT + 2], True, True)],
+       512, ["EQ", "EQ2"] + ["CT" + nm for nm in C], ["bMI"], "cols")
+    op([("s", 0.12, lambda e: e.activation(T.COL[:, 0:NT + 2], T.bMI[:, 0:NT + 2], F.Copy))], [], list(TAB) + ["me", "mo", "bMI"], "cols")
+    iota(col("p"), [[0, 1]], 0, 1, ["p"])
+    for nm, ad in (("q0", 0.0), ("q1", 128.0)):
+        act(col(nm), col("p"), F.Copy, ["p"], [nm], "q", scale=1.0 / 256, bias=ad / 256)
+        act(col(nm), col(nm), F.Square, [nm], [nm], "q")
+        act(col(nm + "b"), col(nm), F.Copy, [nm], [nm + "b"], "q", bias=-1.0)
+    act(T.BASE[:], T.I4B[:], F.Identity, ["I4B", "e12", "c12"], ["BASE"], "base", scale=col("e12"), bias=col("c12"))
 
-    def ci(j):
-        return T.CI[:, j:j + 1]
-    vts(ci(8), T.KI[:], 15, None, A.bitwise_and, None, ["KI"], ["KIt"])
-    vcopy(col("k"), ci(8), ["KIt"], ["k"])
-    for c in range(4):
-        vts(col("e%d" % c), col("k"), float(c), None, A.is_equal, None, ["k"], ["e%d" % c])
-    vtt(col("e02"), col("e0"), col("e2"), A.add, ["e0", "e2"], ["e02"])
-    vtt(col("e13"), col("e1"), col("e3"), A.add, ["e1", "e3"], ["e13"])
-    vts(col("p1"), col("e1"), 256.0, None, A.mult, None, ["e1"], ["p1"])
-    vtt(col("pc"), col("e0"), col("p1"), A.add, ["e0", "p1"], ["pc"])
-    vts(col("pn"), col("pc"), -1.0, None, A.mult, None, ["pc"], ["pn"])
-    for j, fac in enumerate((0.5, 0.25, 0.0625, 0.00390625)):
-        b = 1 << j
-        vts(ci(j), ci(8), b, None, A.bitwise_and, None, ["KIt"], ["ci%d" % j])
-        vts(col("s%d" % j), ci(j), (fac - 1.0) / b, 1.0, A.mult, A.add, ["ci%d" % j], ["s%d" % j])
-    vtt(col("s01"), col("s0"), col("s1"), A.mult, ["s0", "s1"], ["s01"])
-    vtt(col("s23"), col("s2"), col("s3"), A.mult, ["s2", "s3"], ["s23"])
-    vtt(col("sp"), col("s01"), col("s23"), A.mult, ["s01", "s23"], ["sp"])
-    vts(col("sc"), col("sp"), 2048.0, None, A.mult, None, ["sp"], ["sc"])
-    vts(ci(4), T.KI[:], 16, None, A.bitwise_and, None, ["KI"], ["ci4"])
-    vts(col("m0"), ci(4), 0.0625, None, A.mult, None, ["ci4"], ["m0"])
-    vts(col("m1"), col("k"), 12.0, -3.75, A.is_ge, A.mult, ["k"], ["m1"])
-    vts(col("m2"), col("m1"), 1.0, None, A.add, None, ["m1"], ["m2"])
-    vtt(col("mo"), col("m0"), col("m2"), A.mult, ["m0", "m2"], ["mo"])
-    vtt(col("me"), col("m2"), col("mo"), A.subtract, ["m2", "mo"], ["me"])
-    ms(col("c85"), -8.5, ["c85"], half=False)
-    vts(T.RT[:, 0:8], T.SEL[:, 8:16], 256.0, None, A.mult, None, ["SEL"], ["t0"])
-    vtt(T.RT[:, 0:8], T.RT[:, 0:8], T.SEL[:, 0:8], A.add, ["t0", "SEL"], ["P01"])
-    vts(T.RT[:, 8:16], T.SEL[:, 24:32], 256.0, None, A.mult, None, ["SEL"], ["t1"])
-    vtt(T.RT[:, 16:24], T.RT[:, 8:16], T.SEL[:, 16:24], A.add, ["t1", "SEL"], ["P23"])
-    vcopy(T.RHS[:, 0:8], T.BC8[:], ["BC8"], ["RHSa"])
-    vtt(T.RHS[:, 8:16], T.RT[:, 16:24], T.RT[:, 0:8], A.add, ["P23", "P01"], ["RHSb"])
-    vtt(T.RHS[:, 16:24], T.RT[:, 16:24], T.RT[:, 0:8], A.subtract, ["P23", "P01"], ["RHSb"])
-    vtt(T.RHS[:, 24:32], T.RT[:, 16:24], T.RT[:, 0:8], A.subtract, ["P23", "P01"], ["RHSd"])
-    vts(T.RHS[:, 8:24], T.RHS[:, 8:24], 0.5, None, A.mult, None, ["RHSb"], ["RHSb"])
+    def fills(out, vals, W):
+        src, rd = T.ZB[:, 0:8], "ZB"
+        for k, v in vals:
+            aff(out, src, [[-16, 8]], A.not_equal, v, -k, 1, [rd], [W])
+            src, rd = out, W
+    fore[0] = 80.0
+    fills(T.RT[:, 0:8], ((0, 1.0), (1, 256.0)), "P01")
+    fore[0] = 60.0
+    iota(T.WQ1[:], [[0, 2048]], 0, 0, ["WQ1"], ["P01"])
+    fore[0] = 0.0
+    fills(T.RHS[:, 8:16], ((0, 0.5), (1, 128.0), (2, 0.5), (3, 128.0)), "RHSb")
+    fills(T.RHS[:, 16:24], ((0, -1.0), (1, -256.0), (2, 1.0), (3, 256.0)), "RHSd")
+    act(T.RHS[:, 0:8], T.BC8[:], F.Copy, ["BC8"], ["RHSa"], "rhs")
     RH = ["RHSa", "RHSb", "RHSd"]
 
     def fillq(dst, src, R, W):
         op([("s", 16 * (0.065 + 64 * CYC), lambda e: [e.activation(dst[:, 129 * q:128 * q + 128:16], src, F.Copy) for q in range(16)])], R + W, W, "fill")
+    fore[0] = 60.0
     fillq(T.WQP, T.RT[:, 0:8], ["P01"], ["WQP"])
+    fore[0] = 0.0
     fillq(T.WQ1, T.BC8[:], ["BC8"], ["WQ1"])
     vcopy(col("w"), T.wI[:], ["wI"], ["w"])
-    act(T.WQW[:], T.WQ1[:], F.Copy, ["WQ1", "w"], ["WQW"], "WQW", scale=col("w"))
-    vcopy(T.IDB[:], T.IDF[:], ["IDF"], ["IDB"])
-    vts(T.IDN[:], T.IDF[:], -1.0, None, A.mult, None, ["IDF"], ["IDN"])
-    vts(T.I8K[:], T.IDF[:], BIG, None, A.mult, None, ["IDF"], ["I8K"])
-    vts(T.OB[:], T.BLK[:], col("pc"), None, A.mult, None, ["BLK", "pc"], ["OB"], half=True)
-    vts(T.OBN[:], T.BLK[:], col("pn"), None, A.mult, None, ["BLK", "pn"], ["OBN"], half=True)
-    vts(T.DW[:], T.DW[:], col("k"), None, A.add, None, ["DW", "k"], ["DW"])
-    vts(T.NV0[:], T.NV0[:], col("e1"), None, A.add, None, ["NV0", "e1"], ["NV0"])
-    vts(T.NV1[:], T.NV0[:], 512.0, None, A.add, None, ["NV0"], ["NV1"])
-    vts(T.NK[:], T.LOI[:], col("e02"), col("e2"), A.mult, A.add, ["LOI", "e02", "e2"], ["NK"], half=True)
-    vts(T.NKb[:], T.HII[:], col("e13"), None, A.mult, None, ["HII", "e13"], ["NKb"], half=True)
+    op([("s", 1.77, lambda e: e.activation(T.WQW[:], T.WQ1[:], F.Copy, scale=col("w"))),
+        ("v", 0.9, lambda e: e.tensor_scalar(T.WQW[:], T.WQ1[:], col("w"), None, A.mult))], ["WQ1", "w"], ["WQW"], "WQW")
+    act(T.IDB[:], T.IDF[:], F.Copy, ["IDF"], ["IDB"], "cst")
+    act(T.I8K[:], T.IDF[:], F.Copy, ["IDF"], ["I8K"], "cst", scale=BIG)
+    act(T.OB[:], T.BLK[:], F.Copy, ["BLK", "pc"], ["OB"], "cst", scale=col("pc"))
+    act(T.OBN[:], T.BLK[:], F.Copy, ["BLK", "pn"], ["OBN"], "cst", scale=col("pn"))
+    act(T.DW[:], T.DW[:], F.Identity, ["DW", "k"], ["DW"], "cst", bias=col("k"))
+    act(T.NV0[:], T.NV0[:], F.Identity, ["NV0", "e1"], ["NV0"], "cst", bias=col("e1"))
+    act(T.NV1[:], T.NV0[:], F.Copy, ["NV0"], ["NV1"], "cst", bias=512.0)
+    act(T.NK[:], T.LOI[:], F.Identity, ["LOI", "e02", "e2"], ["NK"], "cst", scale=col("e02"), bias=col("e2"))
+    act(T.NKb[:], T.HII[:], F.Copy, ["HII", "e13"], ["NKb"], "cst", scale=col("e13"))
     vtt(T.NK[:], T.NK[:], T.NKb[:], A.add, ["NK", "NKb"], ["NK"])
 
     vcopy(LI(0, 0, 128), T.stI[:], ["stI"], ["L0_0", "L0_1"])
@@ -315,17 +348,15 @@ def rank_program(g, core, T, topo):
     vcopy(T.PDl[:], T.PDt[:], ["PDt"], ["PDl"])
     vcopy(T.PDh[:], T.PDu[:], ["PDu"], ["PDh"])
     DMA(T.PW[0:128:16, :], T.PDl[:], ["PDl"], ["PW0"], "pw0")
-    DMA(T.PW[1:128:16, :], T.PDh[:], ["PDh"], ["PW1"], "pw1", "s")
+    DMA(T.PW[1:128:16, :], T.PDh[:], ["PDh"], ["PW1"], "pw1")
     vts(T.KDt[:], T.KD[:], 255, None, A.bitwise_and, None, ["KD0", "KD1"], ["KDt"])
     vts(T.KDu[:], T.KD[:], 8, None, A.arith_shift_right, None, ["KD0", "KD1"], ["KDu"])
     vcopy(T.KDl[:], T.KDt[:], ["KDt"], ["KDl"])
     vcopy(T.KDh[:], T.KDu[:], ["KDu"], ["KDh"])
     DMA(T.KW[0:128:16, 0:2048], T.KDl[:, 0:128], ["KDl"], ["KW0"], "kw0", kb=32)
-    DMA(T.KW[1:128:16, 0:2048], T.KDh[:, 0:128], ["KDh"], ["KW1"], "kw1", "s", kb=32)
+    DMA(T.KW[1:128:16, 0:2048], T.KDh[:, 0:128], ["KDh"], ["KW1"], "kw1", kb=32)
     DMA(T.KW[2:128:16, 0:2048], T.KDl[:, 128:256], ["KDl"], ["KW2"], "kw2", kb=32)
-    DMA(T.KW[3:128:16, 0:2048], T.KDh[:, 128:256], ["KDh"], ["KW3"], "kw3", "s", kb=32)
-    KWK, KTK = ["KW0", "KW1", "KW2", "KW3"], ["KT0", "KT1", "KT2", "KT3"]
-    DMA(T.ZW[:, 0:2048], T.z[:], ["KDl", "KDh", "PDl", "PDh"], ["ZW"], "z", "y", 512, boost=-100.0)
+    DMA(T.KW[3:128:16, 0:2048], T.KDh[:, 128:256], ["KDh"], ["KW3"], "kw3", kb=32)
     DMA(T.RW[:, 0:2048], T.rs[:], ["KDl", "KDh", "PDl", "PDh"], ["RW"], "rs", "y", 512, boost=-200.0)
     DMA(T.EW[:], T.env[:], ["KDl", "KDh", "PDl", "PDh"], ["EW"], "env", "y", 512, boost=-210.0)
     DMA(T.OW[1:128:16, :], T.HIW[0:8, :], ["HIW", "KDh"], ["OW1"], "ow1", kb=40, boost=-220.0)
@@ -344,14 +375,10 @@ def rank_program(g, core, T, topo):
         off, lk = LI(k, 64 * h, 64 * h + 64), ["L%d_%d" % (k, h)]
         gather(ck[:, 0:HL], T.KW[:, 0:win], off, HL, lk + KWK + (KTK if t else []), ["CKk" + hs], "kid")
         gatherop(ck[:, HL:2 * HL], T.ZW[:, 0:win], off, X[:, HL * h:HL * h + HL], A.is_le, lk + ["ZW", xk] + (["ZT"] if t else []), ["CKz" + hs], "z")
-        PE(lambda e: [e.matmul(tp[:, q:512:16], ck[:, q:2 * HL:16], T.RHS[:], True, True) for q in range(16)], 1024, ["CKk" + hs, "CKz" + hs] + RH, [tk], "T")
+        PE(lambda e: [e.matmul(tp[:, q:384:16], ck[:, q:2 * HL:16], T.RHS[:], True, True) for q in range(16)], 1024, ["CKk" + hs, "CKz" + hs] + RH, [tk], "T")
         ma, mb_, ft = T["MA" + hs], T["MB" + hs], T["FT" + hs]
-        if MS[t][h]:
-            act(ma[:], tp[64:128, 0:128], F.Sign, ["c85"], ["MA" + hs, tk], "m", bias=T.COL[0:64, C["c85"]:C["c85"] + 1])
-        else:
-            vts(ma[:], tp[64:128, 0:128], 8.5, 0.5, A.is_ge, A.subtract, [], ["MA" + hs, tk], "m")
-        dc = 256 if MS[t][h] else 384
-        vtt(mb_[:], ma[:], tp[0:64, dc:dc + 128], A.mult, ["MA" + hs, tk], ["MB" + hs], "t", two=False)
+        vts(ma[:], tp[64:128, 0:128], 8.5, 0.5, A.is_ge, A.subtract, [], ["MA" + hs, tk], "m")
+        vtt(mb_[:], ma[:], tp[0:64, 256:384], A.mult, ["MA" + hs, tk], ["MB" + hs], "t", two=False)
         vtt(ft[:], mb_[:], tp[0:64, 128:256], A.add, ["MB" + hs, tk], ["FT" + hs], "f", two=False)
         PE(lambda e: e.matmul(lp[:, 0:64], ft[:, 0:128], T.IDF[0:64, 0:64], True, True), 256, ["FT" + hs, "IDF"], ["bLP" + hs], "tr")
         vcopy(LI(k + 1, 64 * h, 64 * h + 64), lp[:, 0:64], [], ["L%d_%d" % (k + 1, h), "bLP" + hs], "list")
@@ -392,7 +419,7 @@ def rank_program(g, core, T, topo):
         vts(T.FI[:], T.bMI[:, 0:256], col("sc"), None, A.mult, None, ["sc"], ["FI", "bMI"], "fi")
         vts(T.LF[:], T.bLP0[:, 256:512], 0.0, None, A.is_equal, None, [], ["LF", "bLP0"], "lf")
         vts(T.FB[:], T.FI[:], 2048, None, A.bitwise_and, None, ["FI"], ["FB"], "fb")
-        vts(T.FBI[:], T.FB[:], 1.0 / 1024, -1.0, A.mult, A.add, ["FB"], ["FBI"], "fbi")
+        vtt(T.FBI[:], T.FB[:], T.BASE[:], A.add, ["FB", "BASE"], ["FBI"], "fbi")
         for fx, c in (("FE", "me"), ("FO", "mo")):
             op([("s", 0.28, lambda e, fx=fx, c=c: e.activation(T[fx][:], T.FBI[:], F.Copy, scale=col(c))),
                 ("v", 0.16, lambda e, fx=fx, c=c: e.tensor_scalar(T[fx][:], T.FBI[:], col(c), None, A.mult))], ["FBI", c], [fx], "fx")
@@ -400,29 +427,24 @@ def rank_program(g, core, T, topo):
             p0, fk, bn = 32 * (gr // 2), "FO" if gr % 2 else "FE", ("bTP1", "bSP", "bTP0", "bMI")[gr % 4]
 
             def fn(e, p0=p0, fk=fk, bn=bn):
-                r, bk, fx, fb = [], T[bn], T[fk], T.FBI
-                r.append(e.matmul(bk[:, 0:128], fx[p0:p0 + 32, 0:128], fb[p0:p0 + 32, 0:128], True, False))
-                r.append(e.matmul(bk[:, 0:128], T.IDB[:], T.MASK[:], False, True))
-                r.append(e.matmul(bk[:, 128:256], fx[p0:p0 + 32, 128:256], fb[p0:p0 + 32, 0:128], True, True))
-                r.append(e.matmul(bk[:, 256:384], fx[p0:p0 + 32, 128:256], fb[p0:p0 + 32, 128:256], True, False))
-                r.append(e.matmul(bk[:, 256:384], T.IDB[:], T.MASK[:], False, True))
-                return r
-            PE(fn, 640, [fk, "FBI", "IDB", "MASK"], [bn], "dot")
+                fx, fb = T[fk], T.FBI
+                return [e.matmul(T[bn][:, 0:128], fx[p0:p0 + 32, 0:128], fb[p0:p0 + 32, 0:128], True, True),
+                        e.matmul(T[bn][:, 128:384], fx[p0:p0 + 32, 128:256], fb[p0:p0 + 32, :], True, True)]
+            PE(fn, 384, [fk, "FBI"], [bn], "dot")
 
             def fs(e, bn=bn, gr=gr):
-                return [e.activation(T.JK[:, 512 * (gr % 2) + a:512 * (gr % 2) + b], T[bn][:, a:b], F.Relu, accum_out=T.DM[:, 8 * hf + gr:8 * hf + gr + 1]) for hf, a, b in ((0, 0, 128), (1, 128, 384))]
-
-            def fv(e, bn=bn, gr=gr):
-                return [e.tensor_reduce(T.DM[:, 8 * hf + gr:8 * hf + gr + 1], T[bn][:, a:b], AxisListType.X, A.max) for hf, a, b in ((0, 0, 128), (1, 128, 384))]
-            op([("s", 0.5, fs), ("v", 0.42, fv)], [], ["JK%d" % (gr % 2), "DM%d" % gr, bn], "red")
-        vts(T.DUP[:], T.DM[:], 0.5, None, A.is_ge, None, ["DM%d" % b for b in range(8)], ["DUP"], "dup")
+                return [e.activation(T.JK[:, 512 * (gr % 2) + a:512 * (gr % 2) + b], T[bn][:, a:b], F.Relu, bias=col("q%db" % hf),
+                                     accum_out=T.DM[:, 8 * hf + gr:8 * hf + gr + 1]) for hf, a, b in ((0, 0, 128), (1, 128, 384))]
+            op([("s", 0.5, fs)], ["q0b", "q1b"], ["JK%d" % (gr % 2), "DM%d" % gr, bn], "red")
+        vts(T.DUP[:], T.DM[:], 0.0, None, A.is_gt, None, ["DM%d" % b for b in range(8)], ["DUP"], "dup")
         PE(lambda e: e.matmul(T.bLP1[0:16, 0:128], T.DUP[:], T.IDB[:], True, True), 128, ["DUP", "IDB"], ["bLP1"], "dupT")
-        op([("s", 0.17, lambda e: e.activation(T.DUT[:], T.bLP1[0:16, 0:128], F.Copy)), ("v", 0.16, lambda e: e.tensor_copy(T.DUT[:], T.bLP1[0:16, 0:128]))], [], ["DUT", "bLP1"], "dut")
-        PE(lambda e: [e.matmul(T.bSP[:, 0:256], a_[:], b_, i_ == 0, i_ == 2) for i_, (a_, b_) in enumerate(((T.IDB, T.RF[:]), (T.IDN, T.SS0[:, 0:S]), (T.IDN, T.MM0[:, 0:S])))] +
-           [e.matmul(T.bSP[:, 256:512], T.IDB[:], b_, i_ == 0, i_ == 2) for i_, b_ in enumerate((T.RF[:], T.SS0[:, 0:S], T.MM0[:, 0:S]))],
-           1536, ["IDB", "IDN", "RF", "SS0", "MM0"], ["bSP"], "rv")
-        act(T.AD[:], T.bSP[:, 0:256], F.Abs, [], ["AD", "bSP"], "abs")
-        vcopy(T.RS1[:], T.bSP[:, 256:512], [], ["RS1", "bSP"], "rs1")
+        op([("s", 0.17, lambda e: e.activation(T.DUT[:], T.bLP1[0:16, 0:128], F.Copy)), ("v", 0.16, lambda e: e.tensor_copy(T.DUT[:], T.bLP1[0:16, 0:128]))],
+           [], ["DUT", "bLP1"], "dut")
+        PE(lambda e: [e.matmul(T.bSP[:, 0:256], T.IDB[:], T.SS0[:, 0:S], True, False), e.matmul(T.bSP[:, 0:256], T.IDB[:], T.MM0[:, 0:S], False, True)],
+           512, ["IDB", "SS0", "MM0"], ["bSP"], "vv")
+        vtt(T.DR[:], T.RF[:], T.bSP[:, 0:256], A.subtract, ["RF"], ["DR", "bSP"], "dr", two=False)
+        vtt(T.RS1[:], T.RF[:], T.bSP[:, 0:256], A.add, ["RF", "bSP"], ["RS1"], "rs1", two=False)
+        act(T.AD[:], T.DR[:], F.Abs, ["DR"], ["AD"], "abs")
 
         def fn3(e):
             r = []
@@ -479,7 +501,8 @@ def rank_program(g, core, T, topo):
     vcopy(LI(11, 32, 48), T.SFb[:, 32:48], ["SFb"], ["SFL"])
     gather(T.XF[:], T.XW[:], LI(11, 32, 48), S, ["XW", "SFL"], ["XF"], "xf")
 
-    act(T.EW[:], T.EW[:], F.Copy, ["EW"], ["EW"], "env256", bias=-256.0)
+    op([("s", 1.77, lambda e: e.activation(T.EW[:], T.EW[:], F.Copy, bias=-256.0)),
+        ("v", 0.9, lambda e: e.tensor_scalar(T.EW[:], T.EW[:], -256.0, None, A.add))], ["EW"], ["EW"], "env256")
     outcome(0, T.XS0, ["XS0_0", "XS0_1"])
     for h in range(2):
         hs = str(h)
@@ -494,12 +517,12 @@ def rank_program(g, core, T, topo):
     DMA(T.yr[:, 0:512], T.RW[:, 2048:MW], ["RTa", "RTb"], ["oyr0"], "oyr0")
     vcopy(T.cuF[:], T.cuI[:], ["cuI"], ["cuF"])
     PE(lambda e: e.matmul(T.bLP1[:, 0:128], T.cuF[:], T.IDF[:], True, True), 512, ["cuF", "IDF"], ["bLP1"], "cuT")
-    vcopy(T.cuT[:], T.bLP1[:, 0:128], [], ["cuT", "bLP1"])
+    act(T.cuT[:], T.bLP1[:, 0:128], F.Copy, [], ["cuT", "bLP1"], "cuT")
     for gr in range(8):
         DMA(T.CF[16 * gr:16 * gr + 1, :], T.cuT[:, 16 * gr:16 * gr + 16], ["cuT", "CF"], ["CF%d" % gr], "cf", kb=8)
     send([T.wI[:]], T.wN[:], prv, "aw", "lw", ["wI"], ["wN"], "sendw", 1)
     vcopy(col("wn"), T.wN[:], ["wN"], ["wn"])
-    act(T.WQN[:], T.WQ1[:], F.Copy, ["WQ1", "wn"], ["WQN"], "WQN", scale=col("wn"))
+    act(T.WN8[:], T.BC8[:], F.Copy, ["BC8", "wn"], ["WN8"], "wn8", scale=col("wn"))
 
     for h in range(2):
         hs = str(h)
@@ -511,7 +534,8 @@ def rank_program(g, core, T, topo):
     for k in range(4):
         for h in range(2):
             if k:
-                gather(T["YS%d" % k][:, HL * h:HL * h + HL], T["XS%d" % (k - 1)][:], LI(9, 64 * h, 64 * h + 64), HL, ["XS%d_0" % (k - 1), "XS%d_1" % (k - 1), "LH%d" % h], ["YS%d_%d" % (k, h)], "ys")
+                gather(T["YS%d" % k][:, HL * h:HL * h + HL], T["XS%d" % (k - 1)][:], LI(9, 64 * h, 64 * h + 64), HL,
+                       ["XS%d_0" % (k - 1), "XS%d_1" % (k - 1), "LH%d" % h], ["YS%d_%d" % (k, h)], "ys")
         for h in range(2):
             step(1, k, h, T["YS%d" % k] if k else T.VL, "YS%d_%d" % (k, h) if k else "VL%d" % h)
     for h in range(2):
@@ -523,17 +547,19 @@ def rank_program(g, core, T, topo):
         def fn(e):
             r = []
             for j in range(8):
-                for src in (T["SS%d" % h], T["MM%d" % h]):
-                    q = 128 * (8 * h + j)
-                    r.append(e.matmul(T.bOP0[:, 192:320], T.WQN[:, q:q + 128], src[:, 128 * j:128 * j + 128], h == 0 and not r, h == 1 and len(r) == 15))
+                for a_, src in enumerate((T["SS%d" % h], T["MM%d" % h])):
+                    r.append(e.matmul(T.bOP0[:, 200 + 8 * h + j:328:16], src[:, 128 * j:128 * j + 128], T.WN8[:], a_ == 0, a_ == 1))
             return r
         return fn
     for h in range(2):
-        PE(fnh(h), 2048, ["WQN", "SS%d" % h, "MM%d" % h], ["bOP0"], "hd")
+        PE(fnh(h), 1024, ["WN8", "SS%d" % h, "MM%d" % h], ["bOP0"], "hd")
     i1, i2 = T.IT[:, 256:384], T.IT[:, 384:512]
-    vcopy(i1, T.bOP0[:, 192:320], [], ["HI10", "HI11", "bOP0"], "H1")
+    vcopy(i1, T.bOP0[:, 200:328], [], ["HI10", "HI11", "bOP0"], "H1")
     vts(i2, i1, 2047, None, A.bitwise_and, None, ["HI10", "HI11"], ["HI20", "HI21"], "H2")
-    vts(T.HS[:], i2, 4096.0, None, A.add, None, ["HI20", "HI21"], ["HS"], "H3")
+    vts(T.HFT[:], i2, 4096.0, None, A.add, None, ["HI20", "HI21"], ["HFT"], "H3")
+    PE(lambda e: e.matmul(T.bOP1[:, 256:384], T.HFT[:], T.IDF[:], True, True), 512, ["HFT", "IDF"], ["bOP1"], "HT")
+    op([("s", 0.17, lambda e: e.activation(T.HS[:], T.bOP1[:, 256:384], F.Copy)), ("v", 0.16, lambda e: e.tensor_copy(T.HS[:], T.bOP1[:, 256:384]))],
+       [], ["HS", "bOP1"], "H4")
     send([T.HS[:]], T.HR[:], nxt, "aH", "lH", ["HS"], ["HR"], "sendH", 64)
     DMA(T.yp[:, 2048:4096], T.HR[:], ["HR"], ["oyp2"], "oyp2")
     splits(1)

from concourse.bass import DstId, RemoteDMATransfer
from concourse.mybir import AluOpType as A, ActivationFunctionType as F

S, HL = 256, 1024
MW = 2560
DUMP, WW = 3072, 3328
BIG = 8192.0
BFB, FP, I4, U2 = "bfloat16", "float32", "int32", "uint16"
SCRATCH = {}


def _decl(where, dtype, text):
    for w in text.split():
        nm, c = w.split(":")
        p = 128
        if "x" in c:
            p, c = c.split("x")
        SCRATCH[nm] = (where, [int(p), int(c)], dtype)


_decl("sbuf", BFB, "XW:4096 PW:4096 ZW:3328 KW:3328 RW:2560 EW:2048 OW:2560 HIW:2560 VL:2048 KDl:256 KDh:256 PDl:256 PDh:256 ONB:128 ZB:256 "
      "IDB:128 I8K:128 BC8:8 BLK:128 I4B:256 BASE:256 DR:256 WN8:8 EH:16x256 RHS:24 RT:8 OB:128 OBN:128 WQ1:2048 WQP:2048 WQW:2048 LOI:256 "
      "HII:256 NK:256 NKb:256 YR1:512 XF:256 PT2:256 RF:256 KQ:256 OQ:256 FBI:256 FE:256 FO:256 LF:256 DUP:16 DUT:16x128 JK:1024 AD:256 SP:256 "
      "XS0:2048 XS1:2048 XS2:2048 XS3:2048 YS1:2048 YS2:2048 YS3:2048 CK0:2048 CK1:2048 CR0:1024 CR1:1024 PT0:1024 PT1:1024 SS0:1024 SS1:1024 MM0:1024 MM1:1024")
_decl("sbuf", FP, "KF:3328 CF:2048 HG:2048 thF:8x1 THC:1 KDf:256 cuF:128 cuT:128 ONF:128 IDF:128 E8:8x128 COL:32 CT:32x16 EQ:16x128 EQ2:32x128 DW:16 NV0:256 "
      "NV1:256 FW:80 SW:80 SFa:64 SFb:64 HR:128 HS:128 HFT:128 DM:16 TG:80 A97:128 MA0:64x128 MA1:64x128 MB0:64x128 MB1:64x128 FT0:64x128 FT1:64x128")
_decl("sbuf", I4, "stI:128 cuI:128 KD:256 PD:256 wI:1 wN:1 thI:8x1 KDt:256 KDu:256 PDt:256 PDu:256 FI:256 FB:256 RS1:256 RS2:256 IT:512")
_decl("sbuf", U2, "LL:1536")
_decl("psum", FP, "bMI:512 bSP:512 bTP0:512 bTP1:512 bLP0:512 bLP1:512 bOP0:512 bOP1:512")
SEMAPHORES = ["cv", "cs", "ct", "cg"] + ["d%d" % _k for _k in range(48)] + ["aw", "lw", "aA0", "aA1", "lA0", "lA1", "aH", "lH"]

CYC, GAT = 0.83e-3, 1.56
WAKE, SELF, DBW, DLAT = 0.12, 0.08, 250.0, 2.0
PREF = {"ki": 0, "xs": 0, "pv": 1, "ys": 0, "cu": 0}
BETA, TRIES, PCF, SEED0 = 0.03, 6000, 1.15, 7
MODELS = ((1.2, 1.0, 0.12, 1.0, 1.0), (1.2, 0.72, 0.25, 1.5, 1.3), (1.3, 1.25, 0.1, 0.8, 1.0))
PLANS = {}


def make_plan(ops):
    n = len(ops)
    succ = [[] for _ in range(n)]
    for i, o in enumerate(ops):
        for d in o["deps"]:
            succ[d].append(i)
    rq = [[a[0][0] if a[0] in ("yd", "sd", "gr") else a[0] for a in o["alts"]] for o in ops]
    dma = [o["alts"][0][0] in ("yd", "sd") for o in ops]
    pri = [0.0] * n
    for i in range(n - 1, -1, -1):
        o = ops[i]
        pri[i] = min(a[1] for a in o["alts"]) + o["lat"] + (DLAT if dma[i] else 0.0) + max([pri[j] + WAKE for j in succ[i]] or [0.0])

    def schedule(boost, pick, beta):
        left, ready = [len(o["deps"]) for o in ops], [0.0] * n
        open_ = [i for i in range(n) if not left[i]]
        free, order, bw = {}, [], 0.0
        while open_:
            best = None
            for i in open_:
                p = pri[i] + boost[i]
                for j in range(len(rq[i])):
                    if pick[i] >= 0 and pick[i] != j:
                        continue
                    st = ready[i] if rq[i][j] == "arr" else max(ready[i], free.get(rq[i][j], 0.0))
                    key = (st - beta * p, -p, i, j)
                    if best is None or key < best[0]:
                        best = (key, i, j, st)
            _, i, j, st = best
            open_.remove(i)
            q, d = rq[i][j], ops[i]["alts"][j][1] * (PCF if rq[i][j] in "vstg" else 1.0)
            if q != "arr":
                free[q] = st + d
            fin = st + d + ops[i]["lat"]
            if dma[i]:
                bw = max(bw, st + d) + ops[i]["lat"]
                fin = bw + DLAT
            order.append((i, j))
            for s_ in succ[i]:
                ready[s_] = max(ready[s_], fin + (SELF if rq[s_] == [q] else WAKE))
                left[s_] -= 1
                if not left[s_]:
                    open_.append(s_)
        return order

    def score(order, watch):
        tot, way = 0.0, []
        for mi, (cf, gf, wk, bf, lf) in enumerate(MODELS):
            fin, free, bw, mx, end = [0.0] * n, {}, 0.0, 0.0, 0
            prev, why = {}, [None] * n
            for i, j in order:
                o, q = ops[i], rq[i][j]
                d = o["alts"][j][1]
                if q in "vstg" and not dma[i]:
                    d *= cf * (gf if o["gat"] else 1.0)
                t = 0.0 if q == "arr" else free.get(q, 0.0)
                w = (prev.get(q), True)
                for x in o["deps"]:
                    if fin[x] + wk > t:
                        t = fin[x] + wk
                        w = (x, False)
                why[i], prev[q] = w, i
                e = t + d
                if q != "arr":
                    free[q] = e
                if dma[i]:
                    bw = max(bw, e) + o["lat"] / bf
                    e = bw + DLAT * lf
                else:
                    e += o["lat"] * lf
                fin[i] = e
                if e > mx:
                    mx, end = e, i
            tot += mx / (cf * (1 + gf))
            if mi == watch:
                x = end
                while x is not None:
                    way.append((x, why[x][0] if why[x][1] else None))
                    x = why[x][0]
        return tot, way
    boost, pick = [o["boost"] for o in ops], [o["pref"] for o in ops]
    two = [i for i in range(n) if len(rq[i]) == 2]
    order = schedule(boost, pick, BETA)
    seed = [SEED0]
    best, way = score(order, 0)

    def rnd():
        seed[0] = (seed[0] * 1103515245 + 12345) % 2147483648
        return seed[0] / 2147483648.0
    for it in range(TRIES):
        b2, p2 = list(boost), list(pick)
        share, amp = 0.02 + 0.4 * rnd() ** 2, 1.0 + 12.0 * rnd()
        for i, before in way:
            if before is not None and rnd() < share:
                b2[i] += amp * rnd()
                b2[before] -= amp * rnd()
        if rnd() < 0.5:
            for i in two:
                if rnd() < 0.04:
                    p2[i] = int(3 * rnd()) - 1
        if rnd() < 0.3:
            for i in range(n):
                if rnd() < 0.04:
                    b2[i] += amp * (2 * rnd() - 1)
        o2 = schedule(b2, p2, BETA)
        s2, w2 = score(o2, int(rnd() * len(MODELS)))
        if s2 <= best:
            best, order, boost, pick, way = s2, o2, b2, p2, w2
    return order, best


def rank_program(g, core, T, topo):
    rank = T.rank_of(core)
    if rank is None:
        return
    n_ranks = len(T.cores)
    nxt, prv = T.cores[(rank + 1) % n_ranks], T.cores[(rank - 1) % n_ranks]
    ops, last, readers, fore = [], {}, {}, [0.0]

    def LI(k, a, b):
        return T.LL[:, 128 * k + a:128 * k + b]

    def op(alts, R, W, nm="", lat=0.0, tok=None, boost=0.0, gat=False, pref=-1):
        i, deps = len(ops), set()
        for k in list(R) + list(W):
            if k in last:
                deps.add(last[k])
        for k in W:
            deps.update(readers.get(k, ()))
        for k in R:
            readers.setdefault(k, []).append(i)
        for k in W:
            last[k] = i
            readers[k] = []
        deps.discard(i)
        ops.append(dict(alts=alts, deps=deps, nm=nm, lat=lat, tok=tok, boost=boost + (fore[0] if alts[0][0] in "vstg" else 0.0), gat=gat, pref=pref))

    def vc(n, half=False):
        return 0.05 + max(64, n * (0.5 if half else 1)) * CYC

    def PE(fn, cyc, R, W, nm=""):
        op([("t", 0.05 + cyc * CYC, fn)], R, W, nm)
    nd = [0]

    def DMA(out, in_, R, W, nm="", q="y", kb=64, boost=0.0):
        s = "d%d" % nd[0]
        nd[0] += 1
        op([(q + "d", 0.07, lambda e: e.dma_start(out, in_).then_inc(T.sem[s], 16))], R, W, nm, lat=kb / DBW, tok=(s, 16), boost=boost)

    def vcopy(out, in_, R, W, nm=""):
        op([("v", vc(out.shape[1]), lambda e: e.tensor_copy(out, in_))], R, W, nm)

    def vts(out, in0, s1, s2, o0, o1, R, W, nm="", half=False):
        if o1 is None:
            op([("v", vc(out.shape[1], half), lambda e: e.tensor_scalar(out, in0, s1, None, o0))], R, W, nm)
        else:
            op([("v", vc(out.shape[1], half), lambda e: e.tensor_scalar(out, in0, s1, s2, o0, o1))], R, W, nm)

    def vtt(out, i0, i1, o, R, W, nm="", two=True):
        op([("v", vc(out.shape[1] * (2 if two else 1)), lambda e: e.tensor_tensor(out, i0, i1, o))], R, W, nm)

    def act(out, in_, func, R, W, nm="", **k):
        op([("s", 0.065 + max(64, in_.shape[1]) * CYC, lambda e: e.activation(out, in_, func, **k))], R, W, nm)

    def gather(out, win, off, n, R, W, nm):
        d = n * GAT * CYC
        a = [("s", 0.07 + d, lambda e: e.activation(out, win.indirect(off), F.Copy)),
             ("v", 0.06 + d, lambda e: e.tensor_copy(out, win.indirect(off)))]
        op(a, R, W, nm, gat=True, pref=PREF.get(nm[:2], -1))

    def gatherop(out, win, off, in1, o, R, W, nm):
        op([("v", 0.06 + HL * GAT * CYC, lambda e: e.tensor_tensor(out, win.indirect(off), in1, o))], R, W, nm, gat=True)

    def ms(ap, c, W, half=True):
        op([("v", vc(ap.shape[1], half), lambda e: e.memset(ap, c))], [], W, "ms")

    def cnt_(pat):
        n = 1
        for a_, b_ in pat:
            n *= b_
        return 0.15 + 2 * n * CYC

    def aff(out, in_, pat, cmpo, fill, base, cm, R, W):
        op([("g", cnt_(pat), lambda e: e.affine_select(out, in_, pat, cmpo, fill, base, cm))], R, W)

    def iota(out, pat, base, cm, W, R=()):
        op([("g", cnt_(pat), lambda e: e.iota(out, pat, base, cm, allow_small_or_imprecise_dtypes=True))], R, W)

    B, KWK, KTK = 90.0, ["KW0", "KW1", "KW2", "KW3"], ["KT0", "KT1", "KT2", "KT3"]
    DMA(T.KD[:, 0:128], T.kid0[:], [], ["KD0"], "kid0", "y", boost=B)
    DMA(T.PD[:], T.prev[:], [], ["PD"], "prev", "s", 128, boost=B)
    DMA(T.KD[:, 128:256], T.kid1[:], [], ["KD1"], "kid1", "y", boost=B - 1)
    DMA(T.cuI[:], T.cur[:], [], ["cuI"], "cur", "s", boost=B - 1)
    DMA(T.stI[:], T.start[:], [], ["stI"], "start", "y", boost=B - 2)
    DMA(T.XW[:], T.x[:], [], ["XW"], "x", "s", 1024, boost=B - 60)
    DMA(T.ZW[:, 0:2048], T.z[:], [], ["ZW"], "z", "y", 512, boost=B - 70)
    DMA(T.wI[:], T.w[:], [], ["wI"], "w", "y", 1, boost=B - 3)
    DMA(T.thI[:], T.th[:], [], ["thI"], "th", "y", 1, boost=B - 7)

    fore[0] = 80.0
    ms(T.ONB[:], 1.0, ["ONB"])
    ms(T.ZB[:], 0.0, ["ZB"])
    ms(T.WQP[:], 0.0, ["WQP"])
    fore[0] = 0.0
    ms(T.PW[:], 0.0, ["PW0", "PW1"])
    fore[0] = 60.0
    act(T.KW[:, 0:2048], T.WQP[:], F.Copy, ["WQP"], KWK, "zero")
    fore[0] = 0.0
    ms(T.ONF[:], 1.0, ["ONF"], half=False)
    ms(T.ZW[:, 2048:MW], 0.0, ["ZT"])
    fore[0] = 70.0
    aff(T.BC8[:], T.ONB[:, 0:8], [[-16, 8]], A.is_ge, 0.0, 0, 1, ["ONB"], ["BC8"])
    aff(T.BC8[:], T.BC8[:], [[16, 8]], A.is_ge, 0.0, 15, -1, ["BC8"], ["BC8"])
    fore[0] = 0.0
    aff(T.IDF[:], T.ONF[:], [[-1, 128]], A.is_equal, 0.0, 0, 1, ["ONF"], ["IDF"])
    aff(T.BLK[:], T.ONB[:], [[-16, 8], [0, 16]], A.is_ge, 0.0, 0, 1, ["ONB"], ["BLK"])
    aff(T.BLK[:], T.BLK[:], [[16, 8], [0, 16]], A.is_ge, 0.0, 15, -1, ["BLK"], ["BLK"])
    iota(T.KW[:, 2048:MW], [[0, MW - 2048]], 0, 0, KTK)
    fore[0] = -60.0
    iota(T.OW[:], [[0, 10], [1, 256]], 0, 0, ["OW0", "OW1"])
    iota(T.HIW[:], [[1, 10], [0, 256]], 0, 0, ["HIW"])
    fore[0] = 0.0
    iota(T.I4B[:], [[4, 256]], 0, 0, ["I4B"])
    aff(T.EH[:], T.ZB[0:16, :], [[-8, 2], [-1, 8], [0, 16]], A.not_equal, -BIG, 0, 1, ["ZB"], ["EH"])
    aff(T.E8[:], T.ONF[0:8, :], [[-1, 8], [0, 16]], A.is_equal, 0.0, 0, 1, ["ONF"], ["E8"])
    iota(T.DW[:], [[16, 16]], DUMP, 0, ["DW"])
    iota(T.NV0[:], [[2, 256]], 2048, 0, ["NV0"])
    iota(T.LOI[:], [[0, 2], [2, 128]], 0, 0, ["LOI"])
    iota(T.HII[:], [[1, 2], [0, 128]], 8, 0, ["HII"])
    fore[0] = -60.0
    iota(T.KF[:, 2048:3072], [[1, 1024]], 2048, 0, ["KFt"])
    iota(T.CF[:], [[0, 2048]], 0, 0, ["CF"])

    TAB = {"k": (), "e1": ((1, 1),), "e2": ((2, 1),), "e02": ((0, 1), (2, 1)), "e13": ((1, 1), (3, 1)), "pc": ((0, 1), (1, 256)),
           "pn": ((0, -1), (1, -256)), "sc": tuple((k, 2 ** (11 - k)) for k in range(12)), "e12": ((12, 1),), "c12": ()}
    NT = len(TAB)
    C = dict((nm, j) for j, nm in enumerate(list(TAB) + ["me", "mo", "q0b", "q1b", "p", "q0", "q1", "w", "wn"]))

    def col(nm):
        return T.COL[:, C[nm]:C[nm] + 1]
    fore[0] = 40.0
    ms(T.CT[:], 0.0, ["CT" + nm for nm in C], half=False)
    fore[0] = 0.0
    for nm in TAB:
        c, ck = T.CT[0:16, C[nm]:C[nm] + 1], ["CT" + nm]
        if nm == "k":
            iota(c, [[0, 1]], 0, 1, ck)
        if nm == "c12":
            aff(c, c, [[0, 1]], A.is_equal, -1024.0, -12, 1, ck, ck)
        for k, v in TAB[nm]:
            aff(c, c, [[0, 1]], A.not_equal, float(v), -k, 1, ck, ck)
    u = 2.0 ** -20
    for nm, o in (("me", 0), ("mo", 16)):
        c, ck = T.CT[:, C[nm]:C[nm] + 1], ["CT" + nm]
        aff(c, c, [[0, 1]], A.is_gt, u, 16 if o else -11, -1 if o else 1, ck, ck)
        for k, v in ((12, -u), (13, -5.5 * u), (14, -5.5 * u)) + (((15, 0.0),) if o else ()):
            aff(c, c, [[0, 1]], A.not_equal, v, -k - o, 1, ck, ck)
    aff(T.EQ[:], T.ONF[0:16, :], [[0, 8], [1, 16]], A.is_equal, 0.0, 0, -1, ["ONF"], ["EQ"])
    aff(T.EQ2[:], T.ONF[0:32, :], [[0, 4], [1, 32]], A.is_equal, 0.0, 0, -1, ["ONF"], ["EQ2"])
    PE(lambda e: [e.matmul(T.bMI[:, 0:NT], T.EQ[:], T.CT[0:16, 0:NT], True, True), e.matmul(T.bMI[:, NT:NT + 2], T.EQ2[:], T.CT[:, NT:NT + 2], True, True)],
       512, ["EQ", "EQ2"] + ["CT" + nm for nm in C], ["bMI"], "cols")
    op([("s", 0.12, lambda e: e.activation(T.COL[:, 0:NT + 2], T.bMI[:, 0:NT + 2], F.Copy))], [], list(TAB) + ["me", "mo", "bMI"], "cols")
    iota(col("p"), [[0, 1]], 0, 1, ["p"])
    for nm, ad in (("q0", 0.0), ("q1", 128.0)):
        act(col(nm), col("p"), F.Copy, ["p"], [nm], "q", scale=1.0 / 256, bias=ad / 256)
        act(col(nm), col(nm), F.Square, [nm], [nm], "q")
        act(col(nm + "b"), col(nm), F.Copy, [nm], [nm + "b"], "q", bias=-1.0)
    act(T.BASE[:], T.I4B[:], F.Identity, ["I4B", "e12", "c12"], ["BASE"], "base", scale=col("e12"), bias=col("c12"))

    def fills(out, vals, W):
        src, rd = T.ZB[:, 0:8], "ZB"
        for k, v in vals:
            aff(out, src, [[-16, 8]], A.not_equal, v, -k, 1, [rd], [W])
            src, rd = out, W
    fore[0] = 80.0
    fills(T.RT[:, 0:8], ((0, 1.0), (1, 256.0)), "P01")
    fore[0] = 60.0
    iota(T.WQ1[:], [[0, 2048]], 0, 0, ["WQ1"], ["P01"])
    fore[0] = 0.0
    fills(T.RHS[:, 8:16], ((0, 0.5), (1, 128.0), (2, 0.5), (3, 128.0)), "RHSb")
    fills(T.RHS[:, 16:24], ((0, -1.0), (1, -256.0), (2, 1.0), (3, 256.0)), "RHSd")
    act(T.RHS[:, 0:8], T.BC8[:], F.Copy, ["BC8"], ["RHSa"], "rhs")
    RH = ["RHSa", "RHSb", "RHSd"]

    def fillq(dst, src, R, W):
        op([("s", 16 * (0.065 + 64 * CYC), lambda e: [e.activation(dst[:, 129 * q:128 * q + 128:16], src, F.Copy) for q in range(16)])], R + W, W, "fill")
    fore[0] = 60.0
    fillq(T.WQP, T.RT[:, 0:8], ["P01"], ["WQP"])
    fore[0] = 0.0
    fillq(T.WQ1, T.BC8[:], ["BC8"], ["WQ1"])
    vcopy(col("w"), T.wI[:], ["wI"], ["w"])
    op([("s", 1.77, lambda e: e.activation(T.WQW[:], T.WQ1[:], F.Copy, scale=col("w"))),
        ("v", 0.9, lambda e: e.tensor_scalar(T.WQW[:], T.WQ1[:], col("w"), None, A.mult))], ["WQ1", "w"], ["WQW"], "WQW")
    act(T.IDB[:], T.IDF[:], F.Copy, ["IDF"], ["IDB"], "cst")
    act(T.I8K[:], T.IDF[:], F.Copy, ["IDF"], ["I8K"], "cst", scale=BIG)
    act(T.OB[:], T.BLK[:], F.Copy, ["BLK", "pc"], ["OB"], "cst", scale=col("pc"))
    act(T.OBN[:], T.BLK[:], F.Copy, ["BLK", "pn"], ["OBN"], "cst", scale=col("pn"))
    act(T.DW[:], T.DW[:], F.Identity, ["DW", "k"], ["DW"], "cst", bias=col("k"))
    act(T.NV0[:], T.NV0[:], F.Identity, ["NV0", "e1"], ["NV0"], "cst", bias=col("e1"))
    act(T.NV1[:], T.NV0[:], F.Copy, ["NV0"], ["NV1"], "cst", bias=512.0)
    act(T.NK[:], T.LOI[:], F.Identity, ["LOI", "e02", "e2"], ["NK"], "cst", scale=col("e02"), bias=col("e2"))
    act(T.NKb[:], T.HII[:], F.Copy, ["HII", "e13"], ["NKb"], "cst", scale=col("e13"))
    vtt(T.NK[:], T.NK[:], T.NKb[:], A.add, ["NK", "NKb"], ["NK"])

    vcopy(LI(0, 0, 128), T.stI[:], ["stI"], ["L0_0", "L0_1"])
    vcopy(LI(5, 0, 128), T.cuI[:], ["cuI"], ["SL0_0", "SL0_1"])
    vts(T.PDt[:], T.PD[:], 255, None, A.bitwise_and, None, ["PD"], ["PDt"])
    vts(T.PDu[:], T.PD[:], 8, None, A.arith_shift_right, None, ["PD"], ["PDu"])
    vcopy(T.PDl[:], T.PDt[:], ["PDt"], ["PDl"])
    vcopy(T.PDh[:], T.PDu[:], ["PDu"], ["PDh"])
    DMA(T.PW[0:128:16, :], T.PDl[:], ["PDl"], ["PW0"], "pw0")
    DMA(T.PW[1:128:16, :], T.PDh[:], ["PDh"], ["PW1"], "pw1")
    vts(T.KDt[:], T.KD[:], 255, None, A.bitwise_and, None, ["KD0", "KD1"], ["KDt"])
    vts(T.KDu[:], T.KD[:], 8, None, A.arith_shift_right, None, ["KD0", "KD1"], ["KDu"])
    vcopy(T.KDl[:], T.KDt[:], ["KDt"], ["KDl"])
    vcopy(T.KDh[:], T.KDu[:], ["KDu"], ["KDh"])
    DMA(T.KW[0:128:16, 0:2048], T.KDl[:, 0:128], ["KDl"], ["KW0"], "kw0", kb=32)
    DMA(T.KW[1:128:16, 0:2048], T.KDh[:, 0:128], ["KDh"], ["KW1"], "kw1", kb=32)
    DMA(T.KW[2:128:16, 0:2048], T.KDl[:, 128:256], ["KDl"], ["KW2"], "kw2", kb=32)
    DMA(T.KW[3:128:16, 0:2048], T.KDh[:, 128:256], ["KDh"], ["KW3"], "kw3", kb=32)
    DMA(T.RW[:, 0:2048], T.rs[:], ["KDl", "KDh", "PDl", "PDh"], ["RW"], "rs", "y", 512, boost=-200.0)
    DMA(T.EW[:], T.env[:], ["KDl", "KDh", "PDl", "PDh"], ["EW"], "env", "y", 512, boost=-210.0)
    DMA(T.OW[1:128:16, :], T.HIW[0:8, :], ["HIW", "KDh"], ["OW1"], "ow1", kb=40, boost=-220.0)
    DMA(T.KW[0:128:16, 2048:MW], T.OW[0:128:16, 2048:MW], ["OW0"], ["KT0"], "kt0", kb=8, boost=-220.0)
    DMA(T.KW[1:128:16, 2048:MW], T.HIW[0:8, 2048:MW], ["HIW"], ["KT1"], "kt1", kb=8, boost=-220.0)
    DMA(T.KW[2:128:16, 2048:MW], T.OW[0:128:16, 2048:MW], ["OW0"], ["KT2"], "kt2", kb=8, boost=-220.0)
    DMA(T.KW[3:128:16, 2048:MW], T.HIW[0:8, 2048:MW], ["HIW"], ["KT3"], "kt3", kb=8, boost=-220.0)

    def wrap(bank, c0, wq, src, s0, n, R, W, nm):
        PE(lambda e: [e.matmul(bank[:, c0:c0 + n], wq[:, 128 * q:128 * q + 128], src[:, s0 + q:s0 + 16 * n:16], q == 0, q == 15) for q in range(16)],
           16 * max(64, n), R, W, nm)

    def step(t, k, h, X, xk):
        hs, win = str(h), (MW if t else 2048)
        ck, tp, lp, tk = T["CK" + hs], T["bTP" + hs], T["bLP" + hs], "bTP" + hs
        off, lk = LI(k, 64 * h, 64 * h + 64), ["L%d_%d" % (k, h)]
        gather(ck[:, 0:HL], T.KW[:, 0:win], off, HL, lk + KWK + (KTK if t else []), ["CKk" + hs], "kid")
        gatherop(ck[:, HL:2 * HL], T.ZW[:, 0:win], off, X[:, HL * h:HL * h + HL], A.is_le, lk + ["ZW", xk] + (["ZT"] if t else []), ["CKz" + hs], "z")
        PE(lambda e: [e.matmul(tp[:, q:384:16], ck[:, q:2 * HL:16], T.RHS[:], True, True) for q in range(16)], 1024, ["CKk" + hs, "CKz" + hs] + RH, [tk], "T")
        ma, mb_, ft = T["MA" + hs], T["MB" + hs], T["FT" + hs]
        vts(ma[:], tp[64:128, 0:128], 8.5, 0.5, A.is_ge, A.subtract, [], ["MA" + hs, tk], "m")
        vtt(mb_[:], ma[:], tp[0:64, 256:384], A.mult, ["MA" + hs, tk], ["MB" + hs], "t", two=False)
        vtt(ft[:], mb_[:], tp[0:64, 128:256], A.add, ["MB" + hs, tk], ["FT" + hs], "f", two=False)
        PE(lambda e: e.matmul(lp[:, 0:64], ft[:, 0:128], T.IDF[0:64, 0:64], True, True), 256, ["FT" + hs, "IDF"], ["bLP" + hs], "tr")
        vcopy(LI(k + 1, 64 * h, 64 * h + 64), lp[:, 0:64], [], ["L%d_%d" % (k + 1, h), "bLP" + hs], "list")

    def outcome(t, X, xk):
        win = MW if t else 2048
        for h in range(2):
            wrap(T["bOP%d" % h], 0, T.WQW, X, HL * h, 64, ["WQW", xk[h]], ["bOP%d" % h], "wc")
        for h in range(2):
            hs = str(h)
            bo, cr, ss, mm = T["bOP" + hs], T["CR" + hs], T["SS" + hs], T["MM" + hs]
            xh, a97 = X[:, HL * h:HL * h + HL], T.A97[:, 64 * h:64 * h + 64]
            gatherop(cr[:], T.RW[:, 0:win], LI(4, 64 * h, 64 * h + 64), xh, A.is_gt, ["L4_%d" % h, "RW", xk[h]] + (["RTa", "RTb"] if t else []), ["CR" + hs], "R")
            wrap(bo, 128, T.WQ1, cr, 0, 64, ["WQ1", "CR" + hs], ["bOP" + hs], "a")
            i1, i2, ix = T.IT[:, 64 * h:64 * h + 64], T.IT[:, 128 + 64 * h:192 + 64 * h], LI(10, 64 * h, 64 * h + 64)
            act(a97, bo[:, 128:192], F.Copy, [], ["A97" + hs, "bOP" + hs], "a97", scale=97.0)
            vtt(i1, a97, bo[:, 0:64], A.add, ["A97" + hs], ["XI1" + hs, "bOP" + hs], "i1", two=False)
            vts(i2, i1, 2047, None, A.bitwise_and, None, ["XI1" + hs], ["XI2" + hs], "i2")
            vcopy(ix, i2, ["XI2" + hs], ["IX" + hs], "ix")
            gatherop(ss[:], T.EW[:], ix, xh, A.add, ["IX" + hs, "EW", xk[h]], ["SS" + hs], "env")
            vts(mm[:], ss[:], 0.0, 256.0, A.is_lt, A.mult, ["SS" + hs], ["MM" + hs], "mm", half=True)

    def send(srcs, out, dst, rs, ls, R, W, nm, kb):
        rid, pid = topo.addr(dst)[0], topo.addr(dst)[1]
        k = dict(dst_ids=[DstId(rid=rid, pnc=pid)], dma_engine_mask=topo.mask(core, dst), remote_sem=T.sem[rs])
        tr = RemoteDMATransfer(srcs=srcs, dsts=[out], alu_op=1, **k) if len(srcs) > 1 else RemoteDMATransfer(src=srcs[0], dst=out, **k)
        op([("gr", 1.0, lambda e: e.remote_dma_fused([tr], local_sem=T.sem[ls]))], R, [nm], nm, lat=kb / 60.0, tok=(ls, len(topo.engines(core, dst))))
        op([("arr", 0.0, None)], [nm], W, nm + "arr", lat=2.5, tok=(rs, len(topo.engines(prv if dst == nxt else nxt, core))))

    def splits(t):
        win, off = (MW if t else 2048), LI(4, 0, 16)
        gather(T.OQ[:], T.OW[:, 0:win], off, S, ["L4_0", "OW0", "OW1"], ["OQ"], "oq")
        gather(T.KQ[:], T.KW[:, 0:win], off, S, ["L4_0"] + KWK + (KTK if t else []), ["KQ"], "kq")
        gather(T.RF[:], T.RW[:, 0:win], off, S, ["L4_0", "RW"] + (["RTa", "RTb"] if t else []), ["RF"], "rf")
        PE(lambda e: [e.matmul(T.bMI[:, 0:256], T.OB[:], T.OQ[:], True, True)], 256, ["OB", "OQ"], ["bMI"], "FR")
        PE(lambda e: [e.matmul(T.bLP0[:, 256:512], T.OB[:], T.KQ[:], True, False),
                      e.matmul(T.bLP0[:, 256:512], T.OBN[:], T.OQ[:], False, True)], 512, ["OB", "OBN", "OQ", "KQ"], ["bLP0"], "LD")
        vts(T.FI[:], T.bMI[:, 0:256], col("sc"), None, A.mult, None, ["sc"], ["FI", "bMI"], "fi")
        vts(T.LF[:], T.bLP0[:, 256:512], 0.0, None, A.is_equal, None, [], ["LF", "bLP0"], "lf")
        vts(T.FB[:], T.FI[:], 2048, None, A.bitwise_and, None, ["FI"], ["FB"], "fb")
        vtt(T.FBI[:], T.FB[:], T.BASE[:], A.add, ["FB", "BASE"], ["FBI"], "fbi")
        for fx, c in (("FE", "me"), ("FO", "mo")):
            op([("s", 0.28, lambda e, fx=fx, c=c: e.activation(T[fx][:], T.FBI[:], F.Copy, scale=col(c))),
                ("v", 0.16, lambda e, fx=fx, c=c: e.tensor_scalar(T[fx][:], T.FBI[:], col(c), None, A.mult))], ["FBI", c], [fx], "fx")
        for gr in range(8):
            p0, fk, bn = 32 * (gr // 2), "FO" if gr % 2 else "FE", ("bTP1", "bSP", "bTP0", "bMI")[gr % 4]

            def fn(e, p0=p0, fk=fk, bn=bn):
                fx, fb = T[fk], T.FBI
                return [e.matmul(T[bn][:, 0:128], fx[p0:p0 + 32, 0:128], fb[p0:p0 + 32, 0:128], True, True),
                        e.matmul(T[bn][:, 128:384], fx[p0:p0 + 32, 128:256], fb[p0:p0 + 32, :], True, True)]
            PE(fn, 384, [fk, "FBI"], [bn], "dot")

            def fs(e, bn=bn, gr=gr):
                return [e.activation(T.JK[:, 512 * (gr % 2) + a:512 * (gr % 2) + b], T[bn][:, a:b], F.Relu, bias=col("q%db" % hf),
                                     accum_out=T.DM[:, 8 * hf + gr:8 * hf + gr + 1]) for hf, a, b in ((0, 0, 128), (1, 128, 384))]
            op([("s", 0.5, fs)], ["q0b", "q1b"], ["JK%d" % (gr % 2), "DM%d" % gr, bn], "red")
        vts(T.DUP[:], T.DM[:], 0.0, None, A.is_gt, None, ["DM%d" % b for b in range(8)], ["DUP"], "dup")
        PE(lambda e: e.matmul(T.bLP1[0:16, 0:128], T.DUP[:], T.IDB[:], True, True), 128, ["DUP", "IDB"], ["bLP1"], "dupT")
        op([("s", 0.17, lambda e: e.activation(T.DUT[:], T.bLP1[0:16, 0:128], F.Copy)), ("v", 0.16, lambda e: e.tensor_copy(T.DUT[:], T.bLP1[0:16, 0:128]))],
           [], ["DUT", "bLP1"], "dut")
        PE(lambda e: [e.matmul(T.bSP[:, 0:256], T.IDB[:], T.SS0[:, 0:S], True, False), e.matmul(T.bSP[:, 0:256], T.IDB[:], T.MM0[:, 0:S], False, True)],
           512, ["IDB", "SS0", "MM0"], ["bSP"], "vv")
        vtt(T.DR[:], T.RF[:], T.bSP[:, 0:256], A.subtract, ["RF"], ["DR", "bSP"], "dr", two=False)
        vtt(T.RS1[:], T.RF[:], T.bSP[:, 0:256], A.add, ["RF", "bSP"], ["RS1"], "rs1", two=False)
        act(T.AD[:], T.DR[:], F.Abs, ["DR"], ["AD"], "abs")

        def fn3(e):
            r = []
            for hh in range(2):
                o, sl = T.bMI[:, 128 * hh:128 * hh + 128], slice(128 * hh, 128 * hh + 128)
                r.append(e.matmul(o, T.BLK[:], T.AD[:, sl], True, False))
                r.append(e.matmul(o, T.I8K[:], T.LF[:, sl], False, False))
                r.append(e.matmul(o, T.EH[:, sl], T.DUT[:], False, True))
            return r
        PE(fn3, 768, ["BLK", "AD", "I8K", "LF", "EH", "DUT"], ["bMI"], "far")
        vts(T.SP[:], T.bMI[:, 0:256], T.THC[:], None, A.is_ge, None, ["THC"], ["SP", "bMI"], "sp")
        RN, rn, c0 = (T.YR1, "YR1", 0) if t else (T.RW, "RT", 2048)
        vts(T.RS2[:], T.RS1[:], 1, None, A.arith_shift_right, None, ["RS1"], ["RS2"], "rs2")
        vtt(RN[:, c0:c0 + 512:2], T.RF[:], T.SP[:], A.mult, ["RF", "SP"], [rn + "a"], "rna")
        vtt(RN[:, c0 + 1:c0 + 512:2], T.RS2[:], T.SP[:], A.mult, ["RS2", "SP"], [rn + "b"], "rnb")
        wrap(T.bSP, 0, T.WQP, T.SP, 0, 16, ["SP", "WQP"], ["bSP"], "wsp")
        vcopy(T.TG[:, 0:16], LI(4, 0, 16), ["L4_0"], ["TG0"])
        vtt(T.TG[:, 16:32], T.TG[:, 0:16], T.DW[:], A.subtract, ["TG0", "DW"], ["TG1"])
        vts(T.TG[:, 32:48], T.bSP[:, 0:16], 1.0, None, A.is_ge, None, [], ["TG2", "bSP"])
        vtt(T.TG[:, 48:64], T.TG[:, 16:32], T.TG[:, 32:48], A.mult, ["TG1", "TG2"], ["TG3"])
        vtt(T.TG[:, 64:80], T.TG[:, 48:64], T.DW[:], A.add, ["TG3", "DW"], ["TG4"])
        vcopy(LI(11, 0, 16), T.TG[:, 64:80], ["TG4"], ["TGL"])

        def scat(win_, val, R, W, nm):
            op([("v", 0.05 + S * 3.5 * CYC, lambda e: e.tensor_copy(win_.indirect(LI(11, 0, 16)), val))], R + ["TGL"], W, nm)
        if not t:
            scat(T.KW[:], T.NK[:], ["NK"], KWK + KTK, "scK")
            scat(T.ZW[:], T.XF[:], ["XF"], ["ZW", "ZT"], "scZ")
        scat(T.KF[:], (T.NV1 if t else T.NV0)[:], ["NV1" if t else "NV0"], ["KF0", "KF1", "KFt"], "scF")

    for k in range(4):
        for h in range(2):
            gather(T["XS%d" % k][:, HL * h:HL * h + HL], T.XW[:], LI(5 + k, 64 * h, 64 * h + 64), HL, ["XW", "SL%d_%d" % (k, h)], ["XS%d_%d" % (k, h)], "xs")
        for h in range(2):
            if k < 3:
                gather(T["PT%d" % h][:], T.PW[:], LI(5 + k, 64 * h, 64 * h + 64), HL, ["PW0", "PW1", "SL%d_%d" % (k, h)], ["PT%d" % h], "pv")
                wrap(T.bSP, 0, T.WQP, T["PT%d" % h], 0, 64, ["WQP", "PT%d" % h], ["bSP"], "ws")
                vcopy(LI(6 + k, 64 * h, 64 * h + 64), T.bSP[:, 0:64], [], ["SL%d_%d" % (k + 1, h), "bSP"], "slist")
        for h in range(2):
            step(0, k, h, T["XS%d" % k], "XS%d_%d" % (k, h))
    gather(T.PT2[:], T.PW[:], LI(8, 0, 16), S, ["PW0", "PW1", "SL3_0"], ["PT2"], "p4")
    wrap(T.bSP, 0, T.WQP, T.PT2, 0, 16, ["WQP", "PT2"], ["bSP"], "ws4")
    vcopy(T.SW[:, 64:80], T.bSP[:, 0:16], [], ["SW4", "bSP"])
    for k in range(5):
        vcopy(T.FW[:, 16 * k:16 * k + 16], LI(k, 0, 16), ["L%d_0" % k], ["FW%d" % k])
        if k < 4:
            vcopy(T.SW[:, 16 * k:16 * k + 16], LI(5 + k, 0, 16), ["SL%d_0" % k], ["SW%d" % k])
    vtt(T.SFa[:], T.FW[:, 16:80], T.FW[:, 0:64], A.not_equal, ["FW%d" % k for k in range(5)], ["SFa"])
    vtt(T.SFb[:], T.SW[:, 16:80], T.SW[:, 0:64], A.subtract, ["SW%d" % k for k in range(5)], ["SFb"])
    vtt(T.SFa[:], T.SFa[:], T.SFb[:], A.mult, ["SFa", "SFb"], ["SFa"])
    vtt(T.SFb[:, 0:32], T.SFa[:, 0:32], T.SFa[:, 32:64], A.add, ["SFa"], ["SFb"])
    vtt(T.SFa[:, 0:16], T.SFb[:, 0:16], T.SFb[:, 16:32], A.add, ["SFb"], ["SFa"])
    vtt(T.SFb[:, 32:48], T.SFa[:, 0:16], T.SW[:, 0:16], A.add, ["SFa", "SW0"], ["SFb"])
    vcopy(LI(11, 32, 48), T.SFb[:, 32:48], ["SFb"], ["SFL"])
    gather(T.XF[:], T.XW[:], LI(11, 32, 48), S, ["XW", "SFL"], ["XF"], "xf")

    op([("s", 1.77, lambda e: e.activation(T.EW[:], T.EW[:], F.Copy, bias=-256.0)),
        ("v", 0.9, lambda e: e.tensor_scalar(T.EW[:], T.EW[:], -256.0, None, A.add))], ["EW"], ["EW"], "env256")
    outcome(0, T.XS0, ["XS0_0", "XS0_1"])
    for h in range(2):
        hs = str(h)
        send([T["SS" + hs][:], T["MM" + hs][:]], T.VL[:, HL * h:HL * h + HL], nxt, "aA" + hs, "lA" + hs, ["SS" + hs, "MM" + hs], ["VL%d" % h], "send" + hs, 256)
    vcopy(T.thF[:], T.thI[:], ["thI"], ["thF"])
    PE(lambda e: e.matmul(T.bMI[:, 0:1], T.E8[:], T.thF[:], True, True), 256, ["E8", "thF"], ["bMI"], "th")
    vts(T.THC[:], T.bMI[:, 0:1], BIG, None, A.add, None, [], ["THC", "bMI"])
    vcopy(T.KDf[:], T.KD[:], ["KD0", "KD1"], ["KDf"])
    DMA(T.KF[0:128:16, 0:2048], T.KDf[:, 0:128], ["KDf"], ["KF0"], "kf0", boost=-30.0)
    DMA(T.KF[1:128:16, 0:2048], T.KDf[:, 128:256], ["KDf"], ["KF1"], "kf1", boost=-30.0)
    splits(0)
    DMA(T.yr[:, 0:512], T.RW[:, 2048:MW], ["RTa", "RTb"], ["oyr0"], "oyr0")
    vcopy(T.cuF[:], T.cuI[:], ["cuI"], ["cuF"])
    PE(lambda e: e.matmul(T.bLP1[:, 0:128], T.cuF[:], T.IDF[:], True, True), 512, ["cuF", "IDF"], ["bLP1"], "cuT")
    act(T.cuT[:], T.bLP1[:, 0:128], F.Copy, [], ["cuT", "bLP1"], "cuT")
    for gr in range(8):
        DMA(T.CF[16 * gr:16 * gr + 1, :], T.cuT[:, 16 * gr:16 * gr + 16], ["cuT", "CF"], ["CF%d" % gr], "cf", kb=8)
    send([T.wI[:]], T.wN[:], prv, "aw", "lw", ["wI"], ["wN"], "sendw", 1)
    vcopy(col("wn"), T.wN[:], ["wN"], ["wn"])
    act(T.WN8[:], T.BC8[:], F.Copy, ["BC8", "wn"], ["WN8"], "wn8", scale=col("wn"))

    for h in range(2):
        hs = str(h)
        wrap(T["bOP" + hs], 64, T.WQW, T.VL, HL * h, 64, ["WQW", "VL%d" % h], ["bOP" + hs], "wh")
        i1, i2 = T.IT[:, 256 + 64 * h:320 + 64 * h], T.IT[:, 384 + 64 * h:448 + 64 * h]
        vcopy(i1, T["bOP" + hs][:, 64:128], [], ["HI1" + hs, "bOP" + hs], "h1")
        vts(i2, i1, 2047, None, A.bitwise_and, None, ["HI1" + hs], ["HI2" + hs], "h2")
        vcopy(LI(9, 64 * h, 64 * h + 64), i2, ["HI2" + hs], ["LH" + hs], "h3")
    for k in range(4):
        for h in range(2):
            if k:
                gather(T["YS%d" % k][:, HL * h:HL * h + HL], T["XS%d" % (k - 1)][:], LI(9, 64 * h, 64 * h + 64), HL,
                       ["XS%d_0" % (k - 1), "XS%d_1" % (k - 1), "LH%d" % h], ["YS%d_%d" % (k, h)], "ys")
        for h in range(2):
            step(1, k, h, T["YS%d" % k] if k else T.VL, "YS%d_%d" % (k, h) if k else "VL%d" % h)
    for h in range(2):
        gather(T.HG[:, HL * h:HL * h + HL], T.CF[:], LI(9, 64 * h, 64 * h + 64), HL, ["CF"] + ["CF%d" % a for a in range(8)] + ["LH%d" % h], ["HG%d" % h], "cur")
        DMA(T.yp[:, HL * h:HL * h + HL], T.HG[0:128:16, HL * h:HL * h + HL], ["HG%d" % h], ["oyp%d" % h], "oyp", kb=32)
    outcome(1, T.VL, ["VL0", "VL1"])

    def fnh(h):
        def fn(e):
            r = []
            for j in range(8):
                for a_, src in enumerate((T["SS%d" % h], T["MM%d" % h])):
                    r.append(e.matmul(T.bOP0[:, 200 + 8 * h + j:328:16], src[:, 128 * j:128 * j + 128], T.WN8[:], a_ == 0, a_ == 1))
            return r
        return fn
    for h in range(2):
        PE(fnh(h), 1024, ["WN8", "SS%d" % h, "MM%d" % h], ["bOP0"], "hd")
    i1, i2 = T.IT[:, 256:384], T.IT[:, 384:512]
    vcopy(i1, T.bOP0[:, 200:328], [], ["HI10", "HI11", "bOP0"], "H1")
    vts(i2, i1, 2047, None, A.bitwise_and, None, ["HI10", "HI11"], ["HI20", "HI21"], "H2")
    vts(T.HFT[:], i2, 4096.0, None, A.add, None, ["HI20", "HI21"], ["HFT"], "H3")
    PE(lambda e: e.matmul(T.bOP1[:, 256:384], T.HFT[:], T.IDF[:], True, True), 512, ["HFT", "IDF"], ["bOP1"], "HT")
    op([("s", 0.17, lambda e: e.activation(T.HS[:], T.bOP1[:, 256:384], F.Copy)), ("v", 0.16, lambda e: e.tensor_copy(T.HS[:], T.bOP1[:, 256:384]))],
       [], ["HS", "bOP1"], "H4")
    send([T.HS[:]], T.HR[:], nxt, "aH", "lH", ["HS"], ["HR"], "sendH", 64)
    DMA(T.yp[:, 2048:4096], T.HR[:], ["HR"], ["oyp2"], "oyp2")
    splits(1)
    DMA(T.yr[:, 512:1024], T.YR1[:], ["YR1a", "YR1b"], ["oyr1"], "oyr1", kb=128)
    DMA(T.yk0[:], T.KF[0:128:16, 0:3072], ["KF0", "KFt"], ["oyk0"], "oyk0", kb=96)
    DMA(T.yk1[:], T.KF[1:128:16, 0:3072], ["KF1", "KFt"], ["oyk1"], "oyk1", "s", kb=96)

    if "order" not in PLANS:
        PLANS["order"], PLANS["score"] = make_plan(ops)
    eng = {"v": g.vector, "s": g.scalar, "t": g.tensor, "g": g, "y": g.sync}
    cs = {"v": "cv", "s": "cs", "t": "ct", "g": "cg"}
    cnt = dict((s_, 0) for s_ in cs.values())
    known = dict((q, {}) for q in eng)
    total, token = {}, [None] * len(ops)
    for i, j in PLANS["order"]:
        q, d, fn = ops[i]["alts"][j]
        if q == "arr":
            s_, v = ops[i]["tok"]
            token[i] = (s_, v, {s_: v})
            total[s_] = v
            continue
        r = q[0]
        kn, e = known[r], eng[r]
        need = {}
        for dp in ops[i]["deps"]:
            s_, v, ck = token[dp]
            if kn.get(s_, 0) < v and need.get(s_, (0, None))[0] < v:
                need[s_] = (v, ck)
        for s_ in sorted(need, key=lambda s_: (-len(need[s_][1]), s_)):
            v, ck = need[s_]
            if kn.get(s_, 0) >= v:
                continue
            e.wait_ge(T.sem[s_], v)
            for a, b in ck.items():
                if kn.get(a, 0) < b:
                    kn[a] = b
        out = fn(e)
        if q in cs:
            for x in (out if isinstance(out, list) else [out]):
                x.then_inc(T.sem[cs[q]], 1)
                cnt[cs[q]] += 1
            s_, v = cs[q], cnt[cs[q]]
        else:
            s_, v = ops[i]["tok"]
        total[s_] = v
        ck = dict(kn)
        ck[s_] = v
        token[i] = (s_, v, ck)
    for s_ in sorted(total):
        if known["g"].get(s_, 0) < total[s_]:
            g.wait_ge(T.sem[s_], total[s_])
